import numpy as np
import ml_dtypes


def mxq(x, axis, fmt="e4m3"):
    dtype, down = {"e4m3": (ml_dtypes.float8_e4m3fn, 7), "e5m2": (ml_dtypes.float8_e5m2, 14)}[fmt]
    v = np.moveaxis(np.asarray(x, np.float32).astype(ml_dtypes.bfloat16).astype(np.float64), axis, -1)
    blocks = v.reshape(v.shape[:-1] + (-1, 32))
    amax = np.abs(blocks).max(-1, keepdims=True)
    byte = np.maximum(np.where(amax > 0, np.frexp(amax)[1] - 1 + 127, 0) - down, 1)
    scale = np.exp2(byte - 127.0)
    codes = (blocks / scale).astype(np.float32).astype(dtype).astype(np.float64)
    return np.moveaxis((codes * scale).reshape(v.shape), -1, axis)


WIDE = False


def mx_kscale(k):
    if not WIDE:
        return np.ones(k)
    levels = np.array([10, -10, 5, -5, 0])
    if k % 512:
        return np.exp2(np.random.permutation(np.resize(levels, k // 32))).repeat(32)
    a = np.empty((k // 512, 16))
    for p in range(k // 512):
        a[p, :8] = np.random.permutation(np.resize(levels, 8))
        for g in range(8):
            far = levels[np.abs(levels - a[p, g]) >= 10]
            a[p, g + 8] = far[np.random.randint(len(far))]
    return np.exp2(a.ravel()).repeat(32)


def f64(x):
    return np.asarray(x).astype(np.float64)


def striped8(idx):
    return np.concatenate([x.reshape(-1, 16).T for x in idx]).astype(np.uint16)


def runs(offs, k):
    lists = np.stack([offs[16 * r : 16 * r + 16].T.reshape(-1) for r in range(8)]).astype(np.int64)
    return lists[np.arange(k) % 512 // 64]


def pack_weight(w):
    k, n = w.shape
    w = f64(np.asarray(w, np.float32).astype(ml_dtypes.bfloat16)).reshape(k // 32, 32, n)
    amax = np.abs(w).max(1)
    byte = np.clip(np.where(amax > 0, np.frexp(amax)[1] - 1 + 127 - 7, 1), 1, 254)
    scaled = (w * np.exp2(127.0 - byte)[:, None, :]).reshape(k, n).astype(np.float32)
    words = np.ascontiguousarray(scaled.reshape(k // 512, 128, 4, n).transpose(0, 1, 3, 2)).astype(ml_dtypes.float8_e4m3fn).view(np.uint8)
    return words, np.ascontiguousarray(byte.astype(np.uint8).reshape(k // 512, 16, n))


def unpack_weight(words, scales):
    g, p, n, _ = words.shape
    vals = np.ascontiguousarray(words).view(ml_dtypes.float8_e4m3fn).astype(np.float64) * np.repeat(np.exp2(scales.astype(np.float64) - 127.0), 8, axis=1)[..., None]
    return vals.transpose(0, 1, 3, 2).reshape(g * 512, n)


E2M1 = np.array([0.0, 0.5, 1.0, 1.5, 2.0, 3.0, 4.0, 6.0, -0.0, -0.5, -1.0, -1.5, -2.0, -3.0, -4.0, -6.0])


def pack_fp4(w):
    k, n = w.shape
    w = f64(np.asarray(w, np.float32).astype(ml_dtypes.bfloat16)).reshape(k // 32, 32, n)
    amax = np.abs(w).max(1)
    mant, ex = np.frexp(amax / 6.0)
    byte = np.clip(np.where(amax > 0, np.where(mant > 0.5, ex, ex - 1) + 127, 1), 1, 254)
    scaled = (w * np.exp2(127.0 - byte)[:, None, :]).reshape(k, n).astype(np.float32)
    c = np.ascontiguousarray(scaled.reshape(k // 512, 128, 4, n).transpose(0, 1, 3, 2)).astype(ml_dtypes.float4_e2m1fn).view(np.uint8) & 0xF
    words = (c[..., 0::2] | (c[..., 1::2] << 4)).reshape(k // 512, 128, 2 * n)
    return np.ascontiguousarray(words), np.ascontiguousarray(byte.astype(np.uint8).reshape(k // 512, 16, n))


def unpack_fp4(words, scales):
    g, _, n = scales.shape
    words = np.ascontiguousarray(words).reshape(g, 128, n, 2)
    nib = np.empty((g, 128, n, 4), np.uint8)
    nib[..., 0::2] = words & 0xF
    nib[..., 1::2] = words >> 4
    vals = E2M1[nib] * np.repeat(np.exp2(scales.astype(np.float64) - 127.0), 8, axis=1)[..., None]
    return vals.transpose(0, 1, 3, 2).reshape(g * 512, n)


def planes(y):
    n, m = y.shape
    v = y.astype(np.float32).astype(ml_dtypes.bfloat16).astype(np.float64).reshape(n // 32, 32, m)
    top = np.abs(v).max(1)
    byte = np.clip(np.where(top > 0, np.frexp(top)[1] - 1 + 127 - 7, 1), 1, 254)
    codes = (v * np.exp2(127.0 - byte)[:, None, :]).reshape(n, m).astype(np.float32).astype(ml_dtypes.float8_e4m3fn).view(np.uint8)
    words = codes.reshape(n // 512, 128, 4, m).transpose(0, 1, 3, 2)
    return np.ascontiguousarray(words), np.ascontiguousarray(byte.astype(np.uint8).reshape(n // 512, 16, m))


K, T, S, H, C = 512, 2048, 512, 512, 512


def setup_inputs():
    n = np.random.standard_normal
    s = mx_kscale(K)[:, None]
    packed_xT = pack_weight(n((K, T)) * s)
    packed_w1 = pack_fp4(n((K, H)) / np.sqrt(K) / s)
    return {
        "x_words": packed_xT[0],
        "x_scales": packed_xT[1],
        "w1_words": packed_w1[0],
        "w1_scales": packed_w1[1],
        "gs": (np.random.uniform(0.5, 1.5, (K, 1)) / s).astype(np.float32),
        "offs": striped8(np.random.randint(0, T, (8, S))),
        "n1": striped8(np.stack([np.random.permutation(S) for _ in range(8)])),
        "n2": striped8(np.stack([np.random.permutation(S) for _ in range(8)])),
        "cand": striped8(np.random.randint(0, T, (8, C))),
        "n3": striped8(np.stack([np.random.permutation(S) for _ in range(8)])),
        "n4": striped8(np.stack([np.random.permutation(S) for _ in range(8)])),
    }


def reference(x_words, x_scales, w1_words, w1_scales, gs, offs, n1, n2, cand, n3, n4):
    x_cand = unpack_weight(x_words, x_scales)[np.arange(K)[:, None], runs(cand, K)]
    xq = unpack_weight(x_words, x_scales)[np.arange(K)[:, None], runs(offs, K)]
    y = unpack_fp4(w1_words, w1_scales).T @ xq
    pa = y[np.arange(H)[:, None], runs(n1, H)]
    pb = y[np.arange(H)[:, None], runs(n2, H)]
    z = f64(gs) * (np.maximum(np.maximum(y, pa), pb) - (0.5 * (np.minimum(np.minimum(y, pa), pb))))
    s = 0.0625 * ((x_cand.T @ mxq(z, 0, "e4m3")))
    st = np.maximum(s, s[np.arange(C)[:, None], runs(n3, C)])
    out_0 = np.minimum(st, st[np.arange(C)[:, None], runs(n4, C)])
    return (out_0,) + planes(out_0)

@@ -1,0 +1,249 @@
+from contextlib import ExitStack
+
+import concourse.mybir as mybir
+
+F32 = mybir.dt.float32
+BF16 = mybir.dt.bfloat16
+I32 = mybir.dt.int32
+U32 = mybir.dt.uint32
+U16 = mybir.dt.uint16
+U8 = mybir.dt.uint8
+FP8X4 = mybir.dt.float8_e4m3fn_x4
+FP4X4 = mybir.dt.float4_e2m1fn_x4
+ALU = mybir.AluOpType
+COPY = mybir.ActivationFunctionType.Copy
+
+P = 128
+T = 2048
+S = 512
+HALF = 256
+PIECES = ((0, 256), (256, 384), (384, 512))
+FLOPS = 2 * 2 * 512 * 512 * 512
+
+
+def tile_picked_hcandrangehopmn_none_po_kernel(
+    tc, x_words, x_scales, w1_words, w1_scales, gs, offs, n1, n2, cand, n3, n4, out_0, out_1, out_2
+):
+    nc = tc.nc
+    with ExitStack() as ctx:
+        lists = ctx.enter_context(tc.tile_pool(name="lists", bufs=1))
+        keep = ctx.enter_context(tc.tile_pool(name="keep", bufs=1))
+        psum = ctx.enter_context(tc.psum_pool(name="psum", bufs=1))
+
+        def sb(name, shape, dtype):
+            return keep.tile(shape, dtype, name=name, align_bytes=64)
+
+        def load_list(name, src):
+            tile = lists.tile([P, S // 16], U16, name=name)
+            nc.sync.dma_start(tile[:], src)
+            return tile
+
+        xs = sb("xs", [P, T], U8)
+        w1s_raw = sb("w1s_raw", [P, S], U8)
+        q_scales = sb("q_scales", [P, S], U8)
+        c_scales = sb("c_scales", [P, S], U8)
+        w1w_raw = sb("w1w_raw", [P, 2 * S], U8)
+        xw = sb("xw", [P, T], U32)
+        gains = sb("gains", [P, 4], F32)
+        win = [sb(f"win{t}", [P, 2 * S], F32) for t in range(4)]
+        last_plain = sb("last_plain", [P, S], F32)
+
+        nc.scalar.dma_start(xs[:].bitcast(I32), x_scales[0].bitcast(I32).unsqueeze(1).to_broadcast([16, 8, T // 4]))
+        offs_t = load_list("offs_t", offs)
+        nc.scalar.dma_start(w1w_raw[:].bitcast(I32), w1_words[0].bitcast(I32))
+        nc.sync.dma_start(xw[:].bitcast(I32), x_words[0].rearrange("p n t -> p (n t)").bitcast(I32))
+        cand_t = load_list("cand_t", cand)
+        nc.vector.memset(w1s_raw[:].bitcast(I32), 0)
+        nc.vector.memset(q_scales[:].bitcast(I32), 0)
+        nc.vector.memset(c_scales[:].bitcast(I32), 0)
+        nc.vector.memset(win[0][:, S:], 0.0)
+        for q in range(4):
+            nc.scalar.dma_start(w1s_raw[32 * q : 32 * q + 4, :].bitcast(I32), w1_scales[0, 4 * q : 4 * q + 4, :].bitcast(I32))
+        n1_t = load_list("n1_t", n1)
+        n2_t = load_list("n2_t", n2)
+        nc.scalar.dma_start(gains[:], gs.rearrange("(p t) o -> p (t o)", t=4))
+
+        def move_rows(dst, src):
+            for q in range(4):
+                nc.sync.dma_start(dst[32 * q : 32 * q + 4, :].bitcast(I32), src[32 * q : 32 * q + 32 : 8, :].bitcast(I32))
+
+        q_bytes = sb("q_bytes", [P, S], U8)
+        nc.vector.tensor_copy(q_bytes[:], xs[:].indirect(offs_t[:]))
+        move_rows(q_scales, q_bytes)
+
+        w1w = sb("w1w", [P, 2 * S], U8)
+        w1s = sb("w1s", [P, S], U8)
+        nc.vector.tensor_copy(
+            w1w[:].rearrange("p (t m b) -> p t m b", t=4, b=2), w1w_raw[:].rearrange("p (m t b) -> p t m b", t=4, b=2)
+        )
+        nc.vector.tensor_copy(w1s[:].rearrange("p (t m) -> p t m", t=4), w1s_raw[:].rearrange("p (m t) -> p t m", t=4))
+
+        q_words = sb("q_words", [P, S], U32)
+        nc.vector.tensor_copy(q_words[:], xw[:].indirect(offs_t[:]))
+
+        y_plain = [win[1][:, S:], win[2][:, S:], win[3][:, S:], last_plain[:]]
+        for t in range(4):
+            bank = psum.tile([P, S], F32, name=f"y_bank{t}")
+            nc.tensor.matmul_mx(
+                out=bank[:],
+                lhsT=w1w[:, 256 * t : 256 * (t + 1)].bitcast(FP4X4),
+                lhsT_scale=w1s[:, P * t : P * (t + 1)],
+                rhs=q_words[:].bitcast(FP8X4),
+                rhs_scale=q_scales[:],
+                start=True,
+                stop=True,
+            )
+            nc.scalar.copy(win[t][:, :S], bank[:])
+            nc.scalar.copy(y_plain[t], bank[:])
+
+        c_bytes = sb("c_bytes", [P, S], U8)
+        c_bytes_dealt = sb("c_bytes_dealt", [P, S], U8)
+        c_words = sb("c_words", [P, S], U32)
+        c_words_dealt = sb("c_words_dealt", [P, S], U32)
+        nc.vector.tensor_copy(c_bytes[:], xs[:].indirect(cand_t[:]))
+        nc.vector.tensor_copy(c_words[:], xw[:].indirect(cand_t[:]))
+        nc.vector.tensor_copy(
+            c_bytes_dealt[:].rearrange("p (t m) -> p t m", t=4), c_bytes[:].rearrange("p (m t) -> p t m", t=4)
+        )
+        nc.vector.tensor_copy(
+            c_words_dealt[:].rearrange("p (t c i) -> p c t i", t=4, i=4),
+            c_words[:].rearrange("p (c i t) -> p c t i", t=4, i=4),
+        )
+        move_rows(c_scales, c_bytes_dealt)
+        n3_t = load_list("n3_t", n3)
+        n4_t = load_list("n4_t", n4)
+
+        z_bf = [sb(f"z_bf{i}", [P, b - a, 4], BF16) for i, (a, b) in enumerate(PIECES)]
+        z_words = [sb(f"z_words{i}", [P, b - a], U32) for i, (a, b) in enumerate(PIECES)]
+        z_scales = [sb(f"z_scales{i}", [P, b - a], U8) for i, (a, b) in enumerate(PIECES)]
+        s_bank = [psum.tile([P, S], F32, name=f"s_bank{t}") for t in range(4)]
+        uv = [sb(f"uv{t}", [P, 2 * S], F32) for t in range(4)]
+        hi = [sb(f"hi{t}", [P, S], F32) for t in range(4)]
+        lo = [sb(f"lo{t}", [P, S], F32) for t in range(4)]
+        spread = [sb(f"spread{t}", [P, S], F32) for t in range(4)]
+        f = [sb(f"f{t}", [P, S], F32) for t in range(4)]
+        stt = nc.vector.scalar_tensor_tensor
+
+        def diff(t, side):
+            lst = (n1_t, n2_t)[side]
+            nc.vector.tensor_tensor(uv[t][:, side * S : (side + 1) * S], win[t][:].indirect(lst[:]), y_plain[t], ALU.subtract)
+
+        def extremes(t):
+            stt(hi[t][:], uv[t][:, :S], 0.0, uv[t][:, S:], ALU.max, ALU.max)
+            stt(lo[t][:], uv[t][:, :S], 0.0, uv[t][:, S:], ALU.min, ALU.min)
+
+        def combine(t, a, b):
+            stt(spread[t][:, a:b], lo[t][:, a:b], -0.5, hi[t][:, a:b], ALU.mult, ALU.add)
+
+        def finish(t, a, b):
+            stt(f[t][:, a:b], y_plain[t][:, a:b], 0.5, spread[t][:, a:b], ALU.mult, ALU.add)
+
+        def round_z(t, i):
+            a, b = PIECES[i]
+            nc.scalar.activation(z_bf[i][:, :, t], f[t][:, a:b], COPY, scale=gains[:, t : t + 1])
+
+        def score(i):
+            a, b = PIECES[i]
+            nc.vector.quantize_mx(
+                out=z_words[i][:].bitcast(FP8X4), scales=z_scales[i][:], in_=z_bf[i][:].rearrange("p j t -> p (j t)")
+            )
+            for t in range(4):
+                nc.tensor.matmul_mx(
+                    out=s_bank[t][:, a:b],
+                    lhsT=c_words_dealt[:, P * t : P * (t + 1)].bitcast(FP8X4),
+                    lhsT_scale=c_scales[:, P * t : P * (t + 1)],
+                    rhs=z_words[i][:].bitcast(FP8X4),
+                    rhs_scale=z_scales[i][:],
+                    start=True,
+                    stop=True,
+                )
+            nc.scalar.activation(win[0][:, a:b], s_bank[0][:, a:b], COPY, scale=0.0625)
+
+        diff(0, 0)
+        diff(0, 1)
+        diff(1, 0)
+        for t in range(3):
+            extremes(t)
+            diff(t + 1, 1)
+            combine(t, 0, S)
+            if t < 2:
+                diff(t + 2, 0)
+            else:
+                extremes(3)
+            finish(t, 0, S)
+            for i in range(3):
+                round_z(t, i)
+        combine(3, 0, HALF)
+        combine(3, HALF, S)
+        for i, (a, b) in enumerate(PIECES):
+            finish(3, a, b)
+            round_z(3, i)
+        for i in range(3):
+            score(i)
+        for t in range(1, 4):
+            nc.scalar.activation(win[t][:, :S], s_bank[t][:], COPY, scale=0.0625)
+
+        out_rows = out_0.rearrange("(p t) j -> p t j", t=4)
+        out_words = out_1[0].rearrange("p n t -> p (n t)").bitcast(I32)
+        o_bf = [sb(f"o_bf{i}", [P, b - a, 4], BF16) for i, (a, b) in enumerate(PIECES)]
+        o_words = [sb(f"o_words{i}", [P, b - a], U32) for i, (a, b) in enumerate(PIECES)]
+        o_scales = sb("o_scales", [P, S], U8)
+        g3 = sb("g3", [P, 4, S], F32)
+        g4 = sb("g4", [P, 4, S], F32)
+        res = sb("res", [P, 4, S], F32)
+
+        def fetch3(t):
+            nc.vector.tensor_copy(g3[:, t, :], win[t][:].indirect(n3_t[:]))
+
+        def larger(t):
+            nc.vector.tensor_tensor(uv[t][:, :S], win[t][:, :S], g3[:, t, :], ALU.max)
+
+        def fetch4(t, a, b):
+            nc.vector.tensor_copy(g4[:, t, a:b], uv[t][:].indirect(n4_t[:, a // 16 : b // 16]))
+
+        def smaller(t, a, b):
+            nc.vector.tensor_tensor(res[:, t, a:b], uv[t][:, a:b], g4[:, t, a:b], ALU.min)
+            nc.sync.dma_start(out_rows[:, t, a:b], res[:, t, a:b])
+
+        def round_out(t, i):
+            a, b = PIECES[i]
+            nc.scalar.copy(o_bf[i][:, :, t], res[:, t, a:b])
+
+        def hand_on(i):
+            a, b = PIECES[i]
+            nc.vector.quantize_mx(
+                out=o_words[i][:].bitcast(FP8X4), scales=o_scales[:, a:b], in_=o_bf[i][:].rearrange("p j t -> p (j t)")
+            )
+            nc.sync.dma_start(out_words[:, a:b], o_words[i][:].bitcast(I32))
+
+        fetch3(0)
+        fetch3(1)
+        larger(0)
+        fetch3(2)
+        larger(1)
+        fetch4(0, 0, S)
+        fetch3(3)
+        for t in range(3):
+            smaller(t, 0, S)
+            round_out(t, 0)
+            round_out(t, 1)
+            if t < 2:
+                larger(t + 2)
+                fetch4(t + 1, 0, S)
+            if t == 1:
+                fetch4(3, 0, HALF)
+        smaller(3, 0, HALF)
+        round_out(3, 0)
+        fetch4(3, HALF, S)
+        hand_on(0)
+        smaller(3, HALF, S)
+        round_out(3, 1)
+        a, b = PIECES[2]
+        nc.vector.tensor_copy(
+            o_bf[2][:].rearrange("p (c i) t -> p c t i", i=4), res[:, :, a:b].rearrange("p t (c i) -> p c t i", i=4)
+        )
+        hand_on(1)
+        hand_on(2)
+        for q in range(4):
+            queue = nc.sync if q % 2 == 0 else nc.scalar
+            queue.dma_start(out_2[0, 4 * q : 4 * q + 4, :].bitcast(I32), o_scales[32 * q : 32 * q + 4, :].bitcast(I32))

@@ -1,6 +1,7 @@
 from contextlib import ExitStack
 
 import concourse.mybir as mybir
+from concourse.masks import make_identity
 
 F32 = mybir.dt.float32
 BF16 = mybir.dt.bfloat16
@@ -12,6 +13,8 @@ FP8X4 = mybir.dt.float8_e4m3fn_x4
 FP4X4 = mybir.dt.float4_e2m1fn_x4
 ALU = mybir.AluOpType
 COPY = mybir.ActivationFunctionType.Copy
+RELU = mybir.ActivationFunctionType.Relu
+SIGN = mybir.ActivationFunctionType.Sign
 
 P = 128
 T = 2048
@@ -38,85 +41,104 @@ def tile_picked_hcandrangehopmn_none_po_kernel(
             nc.sync.dma_start(tile[:], src)
             return tile
 
-        xs = sb("xs", [P, T], U8)
-        w1s_raw = sb("w1s_raw", [P, S], U8)
+        xs = keep.tile([P, T], U8, name="xs", tag="xs_then_words", align_bytes=64)
+        w1s_raw = keep.tile([P, S], U8, name="w1s_raw", tag="w1s_raw_then_gains", align_bytes=64)
         q_scales = sb("q_scales", [P, S], U8)
         c_scales = sb("c_scales", [P, S], U8)
         w1w_raw = sb("w1w_raw", [P, 2 * S], U8)
         xw = sb("xw", [P, T], U32)
-        gains = sb("gains", [P, 4], F32)
         win = [sb(f"win{t}", [P, 2 * S], F32) for t in range(4)]
         last_plain = sb("last_plain", [P, S], F32)
 
-        nc.scalar.dma_start(xs[:].bitcast(I32), x_scales[0].bitcast(I32).unsqueeze(1).to_broadcast([16, 8, T // 4]))
+        nc.sync.dma_start(w1w_raw[:].bitcast(I32), w1_words[0].bitcast(I32))
+        for b in range(4):
+            rows = w1_scales[0, b:16:4, :].bitcast(I32)
+            nc.scalar.dma_start(w1s_raw[b:P:4, :].bitcast(I32), rows.unsqueeze(1).to_broadcast([4, 8, S // 4]))
         offs_t = load_list("offs_t", offs)
-        nc.scalar.dma_start(w1w_raw[:].bitcast(I32), w1_words[0].bitcast(I32))
-        nc.sync.dma_start(xw[:].bitcast(I32), x_words[0].rearrange("p n t -> p (n t)").bitcast(I32))
+        nc.sync.dma_start(xs[:].bitcast(I32), x_scales[0].bitcast(I32).unsqueeze(1).to_broadcast([16, 8, T // 4]))
         cand_t = load_list("cand_t", cand)
-        nc.vector.memset(w1s_raw[:].bitcast(I32), 0)
+        n1_t = load_list("n1_t", n1)
+        nc.sync.dma_start(xw[:].bitcast(I32), x_words[0].rearrange("p n t -> p (n t)").bitcast(I32))
+        n2_t = load_list("n2_t", n2)
+        n3_t = load_list("n3_t", n3)
+        n4_t = load_list("n4_t", n4)
         nc.vector.memset(q_scales[:].bitcast(I32), 0)
         nc.vector.memset(c_scales[:].bitcast(I32), 0)
         nc.vector.memset(win[0][:, S:], 0.0)
-        for q in range(4):
-            nc.scalar.dma_start(w1s_raw[32 * q : 32 * q + 4, :].bitcast(I32), w1_scales[0, 4 * q : 4 * q + 4, :].bitcast(I32))
-        n1_t = load_list("n1_t", n1)
-        n2_t = load_list("n2_t", n2)
-        nc.scalar.dma_start(gains[:], gs.rearrange("(p t) o -> p (t o)", t=4))
 
-        def move_rows(dst, src):
+        def move_rows(queue, dst, src):
             for q in range(4):
-                nc.sync.dma_start(dst[32 * q : 32 * q + 4, :].bitcast(I32), src[32 * q : 32 * q + 32 : 8, :].bitcast(I32))
-
-        q_bytes = sb("q_bytes", [P, S], U8)
-        nc.vector.tensor_copy(q_bytes[:], xs[:].indirect(offs_t[:]))
-        move_rows(q_scales, q_bytes)
+                queue.dma_start(dst[32 * q : 32 * q + 4, :].bitcast(I32), src[32 * q : 32 * q + 32 : 8, :].bitcast(I32))
 
         w1w = sb("w1w", [P, 2 * S], U8)
         w1s = sb("w1s", [P, S], U8)
         nc.vector.tensor_copy(
-            w1w[:].rearrange("p (t m b) -> p t m b", t=4, b=2), w1w_raw[:].rearrange("p (m t b) -> p t m b", t=4, b=2)
+            w1w[:].bitcast(U16).rearrange("p (t m) -> p t m", t=4), w1w_raw[:].bitcast(U16).rearrange("p (m t) -> p t m", t=4)
         )
         nc.vector.tensor_copy(w1s[:].rearrange("p (t m) -> p t m", t=4), w1s_raw[:].rearrange("p (m t) -> p t m", t=4))
+        gains = keep.tile([P, 4], F32, name="gains", tag="w1s_raw_then_gains", align_bytes=64)
+        nc.sync.dma_start(gains[:], gs.rearrange("(p t) o -> p (t o)", t=4))
+        sign = sb("sign", [P, 4], F32)
+        hi_weight = sb("hi_weight", [P, 4], F32)
+        lo_weight = sb("lo_weight", [P, 4], F32)
+        ratio = sb("ratio", [P, 4], F32)
+        nc.scalar.activation(sign[:], gains[:], SIGN)
+        nc.scalar.activation(hi_weight[:], sign[:], COPY, scale=1.5, bias=0.5)
+        nc.scalar.activation(lo_weight[:], sign[:], COPY, scale=-1.5, bias=0.5)
+        nc.scalar.activation(ratio[:], sign[:], COPY, scale=0.75, bias=-1.25)
+        identity = sb("identity", [P, P], F32)
+        make_identity(nc, identity[:])
+        q_bytes = sb("q_bytes", [P, S], U8)
+        c_bytes = sb("c_bytes", [P, S], U8)
+        nc.vector.tensor_copy(q_bytes[:], xs[:].indirect(offs_t[:]))
+        move_rows(nc.scalar, q_scales, q_bytes)
+        nc.vector.tensor_copy(c_bytes[:], xs[:].indirect(cand_t[:]))
 
-        q_words = sb("q_words", [P, S], U32)
-        nc.vector.tensor_copy(q_words[:], xw[:].indirect(offs_t[:]))
+        c_bytes_dealt = sb("c_bytes_dealt", [P, S], U8)
+        c_first = sb("c_first", [P, P], U32)
+        words = keep.tile([P, 2 * S], U32, name="words", tag="xs_then_words", align_bytes=64)
+        q_words = words[:, :S]
+        c_words = words[:, S:]
+        nc.vector.tensor_copy(
+            c_bytes_dealt[:].rearrange("p (t m) -> p t m", t=4), c_bytes[:].rearrange("p (m t) -> p t m", t=4)
+        )
+        nc.vector.tensor_copy(q_words, xw[:].indirect(offs_t[:]))
 
         y_plain = [win[1][:, S:], win[2][:, S:], win[3][:, S:], last_plain[:]]
-        for t in range(4):
-            bank = psum.tile([P, S], F32, name=f"y_bank{t}")
+        def project(t, a, b, tag):
+            bank = psum.tile([P, b - a], F32, name=f"y_bank{t}_{a}", tag=tag)
             nc.tensor.matmul_mx(
                 out=bank[:],
                 lhsT=w1w[:, 256 * t : 256 * (t + 1)].bitcast(FP4X4),
                 lhsT_scale=w1s[:, P * t : P * (t + 1)],
-                rhs=q_words[:].bitcast(FP8X4),
-                rhs_scale=q_scales[:],
+                rhs=q_words[:, a:b].bitcast(FP8X4),
+                rhs_scale=q_scales[:, a:b],
                 start=True,
                 stop=True,
             )
-            nc.scalar.copy(win[t][:, :S], bank[:])
-            nc.scalar.copy(y_plain[t], bank[:])
+            return bank
 
-        c_bytes = sb("c_bytes", [P, S], U8)
-        c_bytes_dealt = sb("c_bytes_dealt", [P, S], U8)
-        c_words = sb("c_words", [P, S], U32)
-        c_words_dealt = sb("c_words_dealt", [P, S], U32)
-        nc.vector.tensor_copy(c_bytes[:], xs[:].indirect(cand_t[:]))
-        nc.vector.tensor_copy(c_words[:], xw[:].indirect(cand_t[:]))
-        nc.vector.tensor_copy(
-            c_bytes_dealt[:].rearrange("p (t m) -> p t m", t=4), c_bytes[:].rearrange("p (m t) -> p t m", t=4)
-        )
-        nc.vector.tensor_copy(
-            c_words_dealt[:].rearrange("p (t c i) -> p c t i", t=4, i=4),
-            c_words[:].rearrange("p (c i t) -> p c t i", t=4, i=4),
-        )
-        move_rows(c_scales, c_bytes_dealt)
-        n3_t = load_list("n3_t", n3)
-        n4_t = load_list("n4_t", n4)
+        def leave(dst, bank, t):
+            nc.scalar.activation(dst, bank[:], COPY, scale=gains[:, t : t + 1])
 
-        z_bf = [sb(f"z_bf{i}", [P, b - a, 4], BF16) for i, (a, b) in enumerate(PIECES)]
-        z_words = [sb(f"z_words{i}", [P, b - a], U32) for i, (a, b) in enumerate(PIECES)]
-        z_scales = [sb(f"z_scales{i}", [P, b - a], U8) for i, (a, b) in enumerate(PIECES)]
-        s_bank = [psum.tile([P, S], F32, name=f"s_bank{t}") for t in range(4)]
+        first = [project(0, 0, HALF, "bank0"), project(0, HALF, S, "bank4")]
+        for dst in (win[0], y_plain[0]):
+            leave(dst[:, :HALF], first[0], 0)
+            leave(dst[:, HALF:S], first[1], 0)
+        for t in range(1, 4):
+            bank = project(t, 0, S, f"bank{t}")
+            leave(win[t][:, :S], bank, t)
+            leave(y_plain[t], bank, t)
+
+        nc.vector.tensor_copy(c_words, xw[:].indirect(cand_t[:]))
+        nc.vector.tensor_copy(c_first[:], c_words.rearrange("p (m t) -> p m t", t=4)[:, :, 0])
+        move_rows(nc.sync, c_scales, c_bytes_dealt)
+
+        z_bf = [
+            keep.tile([P, b - a, 4], BF16, name=f"z_bf{i}", tag=f"z_bf{i}", align_bytes=64) for i, (a, b) in enumerate(PIECES)
+        ]
+        z_words = sb("z_words", [P, S], U32)
+        z_scales = sb("z_scales", [P, S], U8)
         uv = [sb(f"uv{t}", [P, 2 * S], F32) for t in range(4)]
         hi = [sb(f"hi{t}", [P, S], F32) for t in range(4)]
         lo = [sb(f"lo{t}", [P, S], F32) for t in range(4)]
@@ -124,69 +146,124 @@ def tile_picked_hcandrangehopmn_none_po_kernel(
         f = [sb(f"f{t}", [P, S], F32) for t in range(4)]
         stt = nc.vector.scalar_tensor_tensor
 
-        def diff(t, side):
-            lst = (n1_t, n2_t)[side]
-            nc.vector.tensor_tensor(uv[t][:, side * S : (side + 1) * S], win[t][:].indirect(lst[:]), y_plain[t], ALU.subtract)
+        def diff(t, side, a, b):
+            entries = (n1_t, n2_t)[side][:, a // 16 : b // 16]
+            nc.vector.tensor_tensor(
+                uv[t][:, side * S + a : side * S + b], win[t][:].indirect(entries), y_plain[t][:, a:b], ALU.subtract
+            )
 
-        def extremes(t):
-            stt(hi[t][:], uv[t][:, :S], 0.0, uv[t][:, S:], ALU.max, ALU.max)
-            stt(lo[t][:], uv[t][:, :S], 0.0, uv[t][:, S:], ALU.min, ALU.min)
+        def extremes(t, a, b):
+            stt(hi[t][:, a:b], uv[t][:, a:b], 0.0, uv[t][:, S + a : S + b], ALU.max, ALU.max)
+            stt(lo[t][:, a:b], uv[t][:, a:b], 0.0, uv[t][:, S + a : S + b], ALU.min, ALU.min)
 
         def combine(t, a, b):
-            stt(spread[t][:, a:b], lo[t][:, a:b], -0.5, hi[t][:, a:b], ALU.mult, ALU.add)
+            stt(spread[t][:, a:b], lo[t][:, a:b], ratio[:, t : t + 1], hi[t][:, a:b], ALU.mult, ALU.add)
 
         def finish(t, a, b):
-            stt(f[t][:, a:b], y_plain[t][:, a:b], 0.5, spread[t][:, a:b], ALU.mult, ALU.add)
+            stt(f[t][:, a:b], spread[t][:, a:b], hi_weight[:, t : t + 1], y_plain[t][:, a:b], ALU.mult, ALU.add)
 
         def round_z(t, i):
             a, b = PIECES[i]
-            nc.scalar.activation(z_bf[i][:, :, t], f[t][:, a:b], COPY, scale=gains[:, t : t + 1])
+            nc.scalar.activation(z_bf[i][:, :, t], f[t][:, a:b], COPY, scale=0.5)
 
-        def score(i):
+        sum_bank = [psum.tile([P, 4, P], F32, name=f"sum_bank{c}", tag=f"bank{c}") for c in range(4)]
+        turned = [sb(f"turned{c}", [P, 2, 2 * P], BF16) for c in range(4)]
+        back_bank = [psum.tile([P, 2, 2, P], F32, name=f"back_bank{h}", tag=f"bank{4 + h}") for h in range(2)]
+
+        def add_turned(t, blocks):
+            a, b = blocks[0] * P, (blocks[-1] + 1) * P
+            nc.scalar.activation(spread[t][:, a:b], hi[t][:, a:b], COPY, scale=hi_weight[:, t : t + 1])
+            nc.scalar.activation(f[t][:, a:b], lo[t][:, a:b], COPY, scale=lo_weight[:, t : t + 1])
+            for c in blocks:
+                terms = (y_plain[t], spread[t][:], f[t][:])
+                for n, term in enumerate(terms):
+                    nc.tensor.matmul(
+                        sum_bank[c][:, t, :], term[:, c * P : (c + 1) * P], identity[:],
+                        start=n == 0, stop=n == 2, is_transpose=True,
+                    )
+
+        def turn_back(u, blocks):
+            for c in blocks:
+                nc.scalar.activation(
+                    turned[c][:, u, :].rearrange("j (p e) -> j p e", e=2),
+                    sum_bank[c][:, 2 * u : 2 * u + 2, :].rearrange("j e p -> j p e"),
+                    COPY, scale=0.5,
+                )
+                nc.tensor.transpose(back_bank[c // 2][:, c % 2, u, :], turned[c][:, u, :].bitcast(F32), identity[:])
+
+        def score(t, a, b, tag, candidates):
+            bank = psum.tile([P, b - a], F32, name=f"s_bank{t}_{a}", tag=tag)
+            nc.tensor.matmul_mx(
+                out=bank[:],
+                lhsT=candidates.bitcast(FP8X4),
+                lhsT_scale=c_scales[:, P * t : P * (t + 1)],
+                rhs=z_words[:, a:b].bitcast(FP8X4),
+                rhs_scale=z_scales[:, a:b],
+                start=True,
+                stop=True,
+            )
+            nc.scalar.activation(win[t][:, a:b], bank[:], COPY, scale=-0.0625 if t < 2 else 0.0625)
+
+        def quantise_z(i):
             a, b = PIECES[i]
             nc.vector.quantize_mx(
-                out=z_words[i][:].bitcast(FP8X4), scales=z_scales[i][:], in_=z_bf[i][:].rearrange("p j t -> p (j t)")
+                out=z_words[:, a:b].bitcast(FP8X4), scales=z_scales[:, a:b], in_=z_bf[i][:].rearrange("p j t -> p (j t)")
             )
-            for t in range(4):
-                nc.tensor.matmul_mx(
-                    out=s_bank[t][:, a:b],
-                    lhsT=c_words_dealt[:, P * t : P * (t + 1)].bitcast(FP8X4),
-                    lhsT_scale=c_scales[:, P * t : P * (t + 1)],
-                    rhs=z_words[i][:].bitcast(FP8X4),
-                    rhs_scale=z_scales[i][:],
-                    start=True,
-                    stop=True,
-                )
-            nc.scalar.activation(win[0][:, a:b], s_bank[0][:, a:b], COPY, scale=0.0625)
+            score(0, a, b, f"bank{(6, 7, 0)[i]}", c_first[:])
 
-        diff(0, 0)
-        diff(0, 1)
-        diff(1, 0)
-        for t in range(3):
-            extremes(t)
-            diff(t + 1, 1)
-            combine(t, 0, S)
-            if t < 2:
-                diff(t + 2, 0)
-            else:
-                extremes(3)
-            finish(t, 0, S)
-            for i in range(3):
-                round_z(t, i)
-        combine(3, 0, HALF)
-        combine(3, HALF, S)
-        for i, (a, b) in enumerate(PIECES):
-            finish(3, a, b)
+        def z_pairs(i):
+            return z_bf[i][:].rearrange("p j t -> p (j t)").bitcast(F32).rearrange("p (j u) -> p j u", u=2)
+
+        diff(0, 0, 0, HALF)
+        diff(0, 0, HALF, S)
+        diff(0, 1, 0, S)
+        diff(1, 0, 0, S)
+        extremes(0, 0, S)
+        add_turned(0, range(4))
+        diff(1, 1, 0, S)
+        diff(2, 0, 0, S)
+        extremes(1, 0, S)
+        add_turned(1, range(4))
+        turn_back(0, range(4))
+        for i in (1, 2):
+            nc.scalar.copy(z_pairs(i)[:, :, 0], back_bank[1][:, i - 1, 0, :])
+        diff(2, 1, 0, S)
+        diff(3, 0, 0, HALF)
+        extremes(2, 0, S)
+        add_turned(2, range(2))
+        diff(3, 1, 0, HALF)
+        combine(2, HALF, S)
+        extremes(3, 0, HALF)
+        add_turned(3, range(2))
+        diff(3, 0, HALF, S)
+        finish(2, HALF, S)
+        diff(3, 1, HALF, S)
+        turn_back(1, range(2))
+        round_z(2, 1)
+        nc.scalar.copy(
+            z_pairs(0).rearrange("p (c j) u -> p c j u", c=2), back_bank[0][:].rearrange("p c u j -> p c j u")
+        )
+        round_z(2, 2)
+        extremes(3, *PIECES[1])
+        extremes(3, *PIECES[2])
+        combine(3, *PIECES[1])
+        combine(3, *PIECES[2])
+        for i in (1, 2):
+            finish(3, *PIECES[i])
             round_z(3, i)
         for i in range(3):
-            score(i)
+            quantise_z(i)
+        c_rest = keep.tile([P, 3, P], U32, name="c_rest", tag="z_bf2", align_bytes=64)
+        nc.vector.tensor_copy(
+            c_rest[:].rearrange("p t (c i) -> p c t i", i=4), c_words.rearrange("p (c i t) -> p c t i", t=4, i=4)[:, :, 1:, :]
+        )
         for t in range(1, 4):
-            nc.scalar.activation(win[t][:, :S], s_bank[t][:], COPY, scale=0.0625)
+            score(t, 0, S, f"bank{t}", c_rest[:, t - 1, :])
 
         out_rows = out_0.rearrange("(p t) j -> p t j", t=4)
         out_words = out_1[0].rearrange("p n t -> p (n t)").bitcast(I32)
         o_bf = [sb(f"o_bf{i}", [P, b - a, 4], BF16) for i, (a, b) in enumerate(PIECES)]
-        o_words = [sb(f"o_words{i}", [P, b - a], U32) for i, (a, b) in enumerate(PIECES)]
+        o_words = sb("o_words", [P, S], U32)
         o_scales = sb("o_scales", [P, S], U8)
         g3 = sb("g3", [P, 4, S], F32)
         g4 = sb("g4", [P, 4, S], F32)
@@ -196,54 +273,77 @@ def tile_picked_hcandrangehopmn_none_po_kernel(
             nc.vector.tensor_copy(g3[:, t, :], win[t][:].indirect(n3_t[:]))
 
         def larger(t):
-            nc.vector.tensor_tensor(uv[t][:, :S], win[t][:, :S], g3[:, t, :], ALU.max)
+            nc.vector.tensor_tensor(uv[t][:, :S], win[t][:, :S], g3[:, t, :], ALU.min if t < 2 else ALU.max)
 
         def fetch4(t, a, b):
             nc.vector.tensor_copy(g4[:, t, a:b], uv[t][:].indirect(n4_t[:, a // 16 : b // 16]))
 
         def smaller(t, a, b):
             nc.vector.tensor_tensor(res[:, t, a:b], uv[t][:, a:b], g4[:, t, a:b], ALU.min)
-            nc.sync.dma_start(out_rows[:, t, a:b], res[:, t, a:b])
 
-        def round_out(t, i):
+        def interleave(copy, i):
             a, b = PIECES[i]
-            nc.scalar.copy(o_bf[i][:, :, t], res[:, t, a:b])
+            copy(o_bf[i][:].rearrange("p (c i) t -> p c t i", i=4), res[:, :, a:b].rearrange("p t (c i) -> p c t i", i=4))
+
+        def smaller_by_sums(t):
+            nc.vector.tensor_tensor(g4[:, t, :], uv[t][:].indirect(n4_t[:]), hi[t][:], ALU.subtract)
+            nc.scalar.activation(lo[t][:], g4[:, t, :], RELU)
+            sums = psum.tile([P, 4, P], F32, name=f"out_sum{t}", tag=f"bank{4 + 2 * t}")
+            back = psum.tile([P, 4, P], F32, name=f"out_back{t}", tag=f"bank{5 + 2 * t}")
+            for c in range(4):
+                for n, term in enumerate((hi[t], lo[t])):
+                    nc.tensor.matmul(
+                        sums[:, c, :], term[:, c * P : (c + 1) * P], identity[:], start=n == 0, stop=n == 1, is_transpose=True
+                    )
+            return sums, back
+
+        def turn_out(t, sums, back):
+            nc.scalar.copy(spread[t][:], sums[:].rearrange("j c p -> j (c p)"))
+            for c in range(4):
+                nc.tensor.transpose(back[:, c, :], spread[t][:, c * P : (c + 1) * P], identity[:])
+
+        def store_turned(t, back):
+            nc.scalar.activation(res[:, t, :], back[:].rearrange("p c j -> p (c j)"), COPY, scale=-1.0)
+            nc.sync.dma_start(out_rows[:, t, :], res[:, t, :])
 
         def hand_on(i):
             a, b = PIECES[i]
             nc.vector.quantize_mx(
-                out=o_words[i][:].bitcast(FP8X4), scales=o_scales[:, a:b], in_=o_bf[i][:].rearrange("p j t -> p (j t)")
+                out=o_words[:, a:b].bitcast(FP8X4), scales=o_scales[:, a:b], in_=o_bf[i][:].rearrange("p j t -> p (j t)")
             )
-            nc.sync.dma_start(out_words[:, a:b], o_words[i][:].bitcast(I32))
 
         fetch3(0)
         fetch3(1)
-        larger(0)
+        for t in range(2):
+            larger(t)
+            nc.scalar.copy(hi[t][:], uv[t][:, :S])
         fetch3(2)
-        larger(1)
-        fetch4(0, 0, S)
+        banks = [smaller_by_sums(t) for t in range(2)]
+        for t in range(2):
+            turn_out(t, *banks[t])
+        for t in range(2):
+            store_turned(t, banks[t][1])
+        larger(2)
         fetch3(3)
-        for t in range(3):
-            smaller(t, 0, S)
-            round_out(t, 0)
-            round_out(t, 1)
-            if t < 2:
-                larger(t + 2)
-                fetch4(t + 1, 0, S)
-            if t == 1:
-                fetch4(3, 0, HALF)
-        smaller(3, 0, HALF)
-        round_out(3, 0)
-        fetch4(3, HALF, S)
+        fetch4(2, 0, HALF)
+        larger(3)
+        for i, (a, b) in enumerate(((0, HALF), (HALF, S))):
+            if i == 1:
+                fetch4(2, a, b)
+            else:
+                smaller(2, a, b)
+            fetch4(3, a, b)
+            if i == 1:
+                smaller(2, a, b)
+            smaller(3, a, b)
+            interleave(nc.scalar.copy, i)
+            nc.sync.dma_start(out_rows[:, 2:4, a:b], res[:, 2:4, a:b])
         hand_on(0)
-        smaller(3, HALF, S)
-        round_out(3, 1)
-        a, b = PIECES[2]
-        nc.vector.tensor_copy(
-            o_bf[2][:].rearrange("p (c i) t -> p c t i", i=4), res[:, :, a:b].rearrange("p t (c i) -> p c t i", i=4)
-        )
+        nc.sync.dma_start(out_words[:, :HALF], o_words[:, :HALF].bitcast(I32))
+        interleave(nc.vector.tensor_copy, 2)
         hand_on(1)
         hand_on(2)
+        nc.sync.dma_start(out_words[:, HALF:], o_words[:, HALF:].bitcast(I32))
         for q in range(4):
-            queue = nc.sync if q % 2 == 0 else nc.scalar
+            queue = nc.scalar if q % 2 == 0 else nc.sync
             queue.dma_start(out_2[0, 4 * q : 4 * q + 4, :].bitcast(I32), o_scales[32 * q : 32 * q + 4, :].bitcast(I32))

@@ -19,8 +19,11 @@ SIGN = mybir.ActivationFunctionType.Sign
 P = 128
 T = 2048
 S = 512
-HALF = 256
-PIECES = ((0, 256), (256, 384), (384, 512))
+HALF = S // 2
+TILES = 4
+SCORE_SCALE = 0.0625
+PIECES = ((0, HALF), (HALF, HALF + P), (HALF + P, S))
+HALVES = ((0, HALF), (HALF, S))
 FLOPS = 2 * 2 * 512 * 512 * 512
 
 
@@ -33,21 +36,24 @@ def tile_picked_hcandrangehopmn_none_po_kernel(
         keep = ctx.enter_context(tc.tile_pool(name="keep", bufs=1))
         psum = ctx.enter_context(tc.psum_pool(name="psum", bufs=1))
 
-        def sb(name, shape, dtype):
-            return keep.tile(shape, dtype, name=name, align_bytes=64)
+        def sb(name, shape, dtype, tag=None):
+            return keep.tile(shape, dtype, name=name, tag=tag or name, align_bytes=64)
+
+        def bank_tile(name, shape, bank):
+            return psum.tile(shape, F32, name=name, tag=f"bank{bank}")
 
         def load_list(name, src):
             tile = lists.tile([P, S // 16], U16, name=name)
             nc.sync.dma_start(tile[:], src)
             return tile
 
-        xs = keep.tile([P, T], U8, name="xs", tag="xs_then_words", align_bytes=64)
-        w1s_raw = keep.tile([P, S], U8, name="w1s_raw", tag="w1s_raw_then_gains", align_bytes=64)
+        xs = sb("xs", [P, T], U8, tag="x_scales_then_words")
+        w1s_raw = sb("w1s_raw", [P, S], U8)
         q_scales = sb("q_scales", [P, S], U8)
         c_scales = sb("c_scales", [P, S], U8)
         w1w_raw = sb("w1w_raw", [P, 2 * S], U8)
         xw = sb("xw", [P, T], U32)
-        win = [sb(f"win{t}", [P, 2 * S], F32) for t in range(4)]
+        win = [sb(f"win{t}", [P, 2 * S], F32) for t in range(TILES)]
         last_plain = sb("last_plain", [P, S], F32)
 
         nc.sync.dma_start(w1w_raw[:].bitcast(I32), w1_words[0].bitcast(I32))
@@ -56,9 +62,11 @@ def tile_picked_hcandrangehopmn_none_po_kernel(
             nc.scalar.dma_start(w1s_raw[b:P:4, :].bitcast(I32), rows.unsqueeze(1).to_broadcast([4, 8, S // 4]))
         offs_t = load_list("offs_t", offs)
         nc.sync.dma_start(xs[:].bitcast(I32), x_scales[0].bitcast(I32).unsqueeze(1).to_broadcast([16, 8, T // 4]))
+        x_rows = x_words[0].rearrange("p n t -> p (n t)").bitcast(I32)
+        nc.sync.dma_start(xw[:, : T // 2].bitcast(I32), x_rows[:, : T // 2])
         cand_t = load_list("cand_t", cand)
         n1_t = load_list("n1_t", n1)
-        nc.sync.dma_start(xw[:].bitcast(I32), x_words[0].rearrange("p n t -> p (n t)").bitcast(I32))
+        nc.sync.dma_start(xw[:, T // 2 :].bitcast(I32), x_rows[:, T // 2 :])
         n2_t = load_list("n2_t", n2)
         n3_t = load_list("n3_t", n3)
         n4_t = load_list("n4_t", n4)
@@ -70,24 +78,27 @@ def tile_picked_hcandrangehopmn_none_po_kernel(
             for q in range(4):
                 queue.dma_start(dst[32 * q : 32 * q + 4, :].bitcast(I32), src[32 * q : 32 * q + 32 : 8, :].bitcast(I32))
 
+        def deal(dst, src):
+            nc.vector.tensor_copy(dst.rearrange("p (t m) -> p t m", t=TILES), src.rearrange("p (m t) -> p t m", t=TILES))
+
         w1w = sb("w1w", [P, 2 * S], U8)
         w1s = sb("w1s", [P, S], U8)
-        nc.vector.tensor_copy(
-            w1w[:].bitcast(U16).rearrange("p (t m) -> p t m", t=4), w1w_raw[:].bitcast(U16).rearrange("p (m t) -> p t m", t=4)
-        )
-        nc.vector.tensor_copy(w1s[:].rearrange("p (t m) -> p t m", t=4), w1s_raw[:].rearrange("p (m t) -> p t m", t=4))
-        gains = keep.tile([P, 4], F32, name="gains", tag="w1s_raw_then_gains", align_bytes=64)
-        nc.sync.dma_start(gains[:], gs.rearrange("(p t) o -> p (t o)", t=4))
-        sign = sb("sign", [P, 4], F32)
-        hi_weight = sb("hi_weight", [P, 4], F32)
-        lo_weight = sb("lo_weight", [P, 4], F32)
-        ratio = sb("ratio", [P, 4], F32)
+        deal(w1w[:].bitcast(U16), w1w_raw[:].bitcast(U16))
+        deal(w1s[:], w1s_raw[:])
+
+        gains = sb("gains", [P, TILES], F32)
+        nc.gpsimd.dma_start(gains[:], gs.rearrange("(p t) o -> p (t o)", t=TILES))
+        sign = sb("sign", [P, TILES], F32)
+        hi_weight = sb("hi_weight", [P, TILES], F32)
+        lo_weight = sb("lo_weight", [P, TILES], F32)
+        lo_over_hi = sb("lo_over_hi", [P, TILES], F32)
         nc.scalar.activation(sign[:], gains[:], SIGN)
         nc.scalar.activation(hi_weight[:], sign[:], COPY, scale=1.5, bias=0.5)
         nc.scalar.activation(lo_weight[:], sign[:], COPY, scale=-1.5, bias=0.5)
-        nc.scalar.activation(ratio[:], sign[:], COPY, scale=0.75, bias=-1.25)
+        nc.scalar.activation(lo_over_hi[:], sign[:], COPY, scale=0.75, bias=-1.25)
         identity = sb("identity", [P, P], F32)
         make_identity(nc, identity[:])
+
         q_bytes = sb("q_bytes", [P, S], U8)
         c_bytes = sb("c_bytes", [P, S], U8)
         nc.vector.tensor_copy(q_bytes[:], xs[:].indirect(offs_t[:]))
@@ -96,105 +107,99 @@ def tile_picked_hcandrangehopmn_none_po_kernel(
 
         c_bytes_dealt = sb("c_bytes_dealt", [P, S], U8)
         c_first = sb("c_first", [P, P], U32)
-        words = keep.tile([P, 2 * S], U32, name="words", tag="xs_then_words", align_bytes=64)
+        words = sb("words", [P, 2 * S], U32, tag="x_scales_then_words")
         q_words = words[:, :S]
         c_words = words[:, S:]
-        nc.vector.tensor_copy(
-            c_bytes_dealt[:].rearrange("p (t m) -> p t m", t=4), c_bytes[:].rearrange("p (m t) -> p t m", t=4)
-        )
+        deal(c_bytes_dealt[:], c_bytes[:])
         nc.vector.tensor_copy(q_words, xw[:].indirect(offs_t[:]))
 
         y_plain = [win[1][:, S:], win[2][:, S:], win[3][:, S:], last_plain[:]]
-        def project(t, a, b, tag):
-            bank = psum.tile([P, b - a], F32, name=f"y_bank{t}_{a}", tag=tag)
+
+        def project(t, a, b, bank):
+            acc = bank_tile(f"y{t}_{a}", [P, b - a], bank)
             nc.tensor.matmul_mx(
-                out=bank[:],
-                lhsT=w1w[:, 256 * t : 256 * (t + 1)].bitcast(FP4X4),
+                out=acc[:],
+                lhsT=w1w[:, 2 * P * t : 2 * P * (t + 1)].bitcast(FP4X4),
                 lhsT_scale=w1s[:, P * t : P * (t + 1)],
                 rhs=q_words[:, a:b].bitcast(FP8X4),
                 rhs_scale=q_scales[:, a:b],
                 start=True,
                 stop=True,
             )
-            return bank
+            return acc
 
-        def leave(dst, bank, t):
-            nc.scalar.activation(dst, bank[:], COPY, scale=gains[:, t : t + 1])
+        def leave(dst, acc, t):
+            nc.scalar.activation(dst, acc[:], COPY, scale=gains[:, t : t + 1])
 
-        first = [project(0, 0, HALF, "bank0"), project(0, HALF, S, "bank4")]
+        first = [project(0, 0, HALF, 0), project(0, HALF, S, 4)]
         for dst in (win[0], y_plain[0]):
-            leave(dst[:, :HALF], first[0], 0)
-            leave(dst[:, HALF:S], first[1], 0)
-        for t in range(1, 4):
-            bank = project(t, 0, S, f"bank{t}")
-            leave(win[t][:, :S], bank, t)
-            leave(y_plain[t], bank, t)
+            for (a, b), acc in zip(HALVES, first):
+                leave(dst[:, a:b], acc, 0)
+        for t in range(1, TILES):
+            acc = project(t, 0, S, t)
+            leave(win[t][:, :S], acc, t)
+            leave(y_plain[t], acc, t)
 
         nc.vector.tensor_copy(c_words, xw[:].indirect(cand_t[:]))
-        nc.vector.tensor_copy(c_first[:], c_words.rearrange("p (m t) -> p m t", t=4)[:, :, 0])
+        nc.vector.tensor_copy(c_first[:], c_words.rearrange("p (m t) -> p m t", t=TILES)[:, :, 0])
         move_rows(nc.sync, c_scales, c_bytes_dealt)
 
-        z_bf = [
-            keep.tile([P, b - a, 4], BF16, name=f"z_bf{i}", tag=f"z_bf{i}", align_bytes=64) for i, (a, b) in enumerate(PIECES)
-        ]
+        z_bf = [sb(f"z_bf{i}", [P, b - a, TILES], BF16) for i, (a, b) in enumerate(PIECES)]
         z_words = sb("z_words", [P, S], U32)
         z_scales = sb("z_scales", [P, S], U8)
-        uv = [sb(f"uv{t}", [P, 2 * S], F32) for t in range(4)]
-        hi = [sb(f"hi{t}", [P, S], F32) for t in range(4)]
-        lo = [sb(f"lo{t}", [P, S], F32) for t in range(4)]
-        spread = [sb(f"spread{t}", [P, S], F32) for t in range(4)]
-        f = [sb(f"f{t}", [P, S], F32) for t in range(4)]
+        steps = [sb(f"steps{t}", [P, 2 * S], F32) for t in range(TILES)]
+        hi = [sb(f"hi{t}", [P, S], F32) for t in range(TILES)]
+        lo = [sb(f"lo{t}", [P, S], F32) for t in range(TILES)]
+        term_a = [sb(f"term_a{t}", [P, S], F32) for t in range(TILES)]
+        term_b = [sb(f"term_b{t}", [P, S], F32) for t in range(TILES)]
         stt = nc.vector.scalar_tensor_tensor
 
-        def diff(t, side, a, b):
+        def step(t, side, a, b):
             entries = (n1_t, n2_t)[side][:, a // 16 : b // 16]
             nc.vector.tensor_tensor(
-                uv[t][:, side * S + a : side * S + b], win[t][:].indirect(entries), y_plain[t][:, a:b], ALU.subtract
+                steps[t][:, side * S + a : side * S + b], win[t][:].indirect(entries), y_plain[t][:, a:b], ALU.subtract
             )
 
         def extremes(t, a, b):
-            stt(hi[t][:, a:b], uv[t][:, a:b], 0.0, uv[t][:, S + a : S + b], ALU.max, ALU.max)
-            stt(lo[t][:, a:b], uv[t][:, a:b], 0.0, uv[t][:, S + a : S + b], ALU.min, ALU.min)
+            stt(hi[t][:, a:b], steps[t][:, a:b], 0.0, steps[t][:, S + a : S + b], ALU.max, ALU.max)
+            stt(lo[t][:, a:b], steps[t][:, a:b], 0.0, steps[t][:, S + a : S + b], ALU.min, ALU.min)
 
-        def combine(t, a, b):
-            stt(spread[t][:, a:b], lo[t][:, a:b], ratio[:, t : t + 1], hi[t][:, a:b], ALU.mult, ALU.add)
-
-        def finish(t, a, b):
-            stt(f[t][:, a:b], spread[t][:, a:b], hi_weight[:, t : t + 1], y_plain[t][:, a:b], ALU.mult, ALU.add)
-
-        def round_z(t, i):
-            a, b = PIECES[i]
-            nc.scalar.activation(z_bf[i][:, :, t], f[t][:, a:b], COPY, scale=0.5)
-
-        sum_bank = [psum.tile([P, 4, P], F32, name=f"sum_bank{c}", tag=f"bank{c}") for c in range(4)]
+        sum_bank = [bank_tile(f"sum{c}", [P, TILES, P], c) for c in range(4)]
         turned = [sb(f"turned{c}", [P, 2, 2 * P], BF16) for c in range(4)]
-        back_bank = [psum.tile([P, 2, 2, P], F32, name=f"back_bank{h}", tag=f"bank{4 + h}") for h in range(2)]
+        for c in (2, 3):
+            nc.vector.memset(turned[c][:, 1, :], 0.0)
+        back_bank = [bank_tile(f"back{h}", [P, 2, 2, P], 4 + h) for h in range(2)]
 
-        def add_turned(t, blocks):
-            a, b = blocks[0] * P, (blocks[-1] + 1) * P
-            nc.scalar.activation(spread[t][:, a:b], hi[t][:, a:b], COPY, scale=hi_weight[:, t : t + 1])
-            nc.scalar.activation(f[t][:, a:b], lo[t][:, a:b], COPY, scale=lo_weight[:, t : t + 1])
-            for c in blocks:
-                terms = (y_plain[t], spread[t][:], f[t][:])
-                for n, term in enumerate(terms):
-                    nc.tensor.matmul(
-                        sum_bank[c][:, t, :], term[:, c * P : (c + 1) * P], identity[:],
-                        start=n == 0, stop=n == 2, is_transpose=True,
-                    )
+        def add_turned(acc, terms, c):
+            for n, term in enumerate(terms):
+                nc.tensor.matmul(
+                    acc, term[:, c * P : (c + 1) * P], identity[:], start=n == 0, stop=n == len(terms) - 1, is_transpose=True
+                )
 
-        def turn_back(u, blocks):
-            for c in blocks:
+        def sum_z(t, chunks):
+            a, b = chunks[0] * P, (chunks[-1] + 1) * P
+            nc.scalar.activation(term_a[t][:, a:b], hi[t][:, a:b], COPY, scale=hi_weight[:, t : t + 1])
+            nc.scalar.activation(term_b[t][:, a:b], lo[t][:, a:b], COPY, scale=lo_weight[:, t : t + 1])
+            for c in chunks:
+                add_turned(sum_bank[c][:, t, :], (y_plain[t], term_a[t][:], term_b[t][:]), c)
+
+        def turn_back(u, chunks, members):
+            for c in chunks:
                 nc.scalar.activation(
-                    turned[c][:, u, :].rearrange("j (p e) -> j p e", e=2),
-                    sum_bank[c][:, 2 * u : 2 * u + 2, :].rearrange("j e p -> j p e"),
-                    COPY, scale=0.5,
+                    turned[c][:, u, :].rearrange("j (p e) -> j p e", e=2)[:, :, :members],
+                    sum_bank[c][:, 2 * u : 2 * u + members, :].rearrange("j e p -> j p e"),
+                    COPY,
+                    scale=0.5,
                 )
                 nc.tensor.transpose(back_bank[c // 2][:, c % 2, u, :], turned[c][:, u, :].bitcast(F32), identity[:])
 
-        def score(t, a, b, tag, candidates):
-            bank = psum.tile([P, b - a], F32, name=f"s_bank{t}_{a}", tag=tag)
+        def z_pairs(i):
+            return z_bf[i][:].rearrange("p j t -> p (j t)").bitcast(F32).rearrange("p (j u) -> p j u", u=2)
+
+        def score(t, a, b, bank, candidates):
+            acc = bank_tile(f"s{t}_{a}", [P, b - a], bank)
             nc.tensor.matmul_mx(
-                out=bank[:],
+                out=acc[:],
                 lhsT=candidates.bitcast(FP8X4),
                 lhsT_scale=c_scales[:, P * t : P * (t + 1)],
                 rhs=z_words[:, a:b].bitcast(FP8X4),
@@ -202,147 +207,130 @@ def tile_picked_hcandrangehopmn_none_po_kernel(
                 start=True,
                 stop=True,
             )
-            nc.scalar.activation(win[t][:, a:b], bank[:], COPY, scale=-0.0625 if t < 2 else 0.0625)
+            nc.scalar.activation(win[t][:, a:b], acc[:], COPY, scale=-SCORE_SCALE if t < 2 else SCORE_SCALE)
 
-        def quantise_z(i):
+        step(0, 0, 0, HALF)
+        step(0, 0, HALF, S)
+        step(0, 1, 0, S)
+        step(1, 0, 0, S)
+        extremes(0, 0, S)
+        sum_z(0, range(4))
+        step(1, 1, 0, S)
+        step(2, 0, 0, S)
+        extremes(1, 0, S)
+        sum_z(1, range(4))
+        turn_back(0, range(4), 2)
+        step(2, 1, 0, S)
+        step(3, 0, 0, HALF)
+        extremes(2, 0, S)
+        sum_z(2, range(4))
+        step(3, 1, 0, HALF)
+        step(3, 0, HALF, S)
+        extremes(3, 0, HALF)
+        turn_back(1, (2, 3), 1)
+        sum_z(3, range(2))
+        for i in (1, 2):
+            nc.scalar.copy(z_pairs(i), back_bank[1][:, i - 1, :, :].rearrange("p u j -> p j u"))
+        step(3, 1, HALF, S)
+        turn_back(1, range(2), 2)
+        nc.scalar.copy(z_pairs(0).rearrange("p (c j) u -> p c j u", c=2), back_bank[0][:].rearrange("p c u j -> p c j u"))
+        for a, b in PIECES[1:]:
+            extremes(3, a, b)
+        for a, b in PIECES[1:]:
+            stt(term_a[3][:, a:b], lo[3][:, a:b], lo_over_hi[:, 3:4], hi[3][:, a:b], ALU.mult, ALU.add)
+        for i in (1, 2):
+            a, b = PIECES[i]
+            stt(term_b[3][:, a:b], term_a[3][:, a:b], hi_weight[:, 3:4], y_plain[3][:, a:b], ALU.mult, ALU.add)
+            nc.scalar.activation(z_bf[i][:, :, 3], term_b[3][:, a:b], COPY, scale=0.5)
+        for i, bank in enumerate((6, 7, 0)):
             a, b = PIECES[i]
             nc.vector.quantize_mx(
                 out=z_words[:, a:b].bitcast(FP8X4), scales=z_scales[:, a:b], in_=z_bf[i][:].rearrange("p j t -> p (j t)")
             )
-            score(0, a, b, f"bank{(6, 7, 0)[i]}", c_first[:])
-
-        def z_pairs(i):
-            return z_bf[i][:].rearrange("p j t -> p (j t)").bitcast(F32).rearrange("p (j u) -> p j u", u=2)
-
-        diff(0, 0, 0, HALF)
-        diff(0, 0, HALF, S)
-        diff(0, 1, 0, S)
-        diff(1, 0, 0, S)
-        extremes(0, 0, S)
-        add_turned(0, range(4))
-        diff(1, 1, 0, S)
-        diff(2, 0, 0, S)
-        extremes(1, 0, S)
-        add_turned(1, range(4))
-        turn_back(0, range(4))
-        for i in (1, 2):
-            nc.scalar.copy(z_pairs(i)[:, :, 0], back_bank[1][:, i - 1, 0, :])
-        diff(2, 1, 0, S)
-        diff(3, 0, 0, HALF)
-        extremes(2, 0, S)
-        add_turned(2, range(2))
-        diff(3, 1, 0, HALF)
-        combine(2, HALF, S)
-        extremes(3, 0, HALF)
-        add_turned(3, range(2))
-        diff(3, 0, HALF, S)
-        finish(2, HALF, S)
-        diff(3, 1, HALF, S)
-        turn_back(1, range(2))
-        round_z(2, 1)
-        nc.scalar.copy(
-            z_pairs(0).rearrange("p (c j) u -> p c j u", c=2), back_bank[0][:].rearrange("p c u j -> p c j u")
-        )
-        round_z(2, 2)
-        extremes(3, *PIECES[1])
-        extremes(3, *PIECES[2])
-        combine(3, *PIECES[1])
-        combine(3, *PIECES[2])
-        for i in (1, 2):
-            finish(3, *PIECES[i])
-            round_z(3, i)
-        for i in range(3):
-            quantise_z(i)
-        c_rest = keep.tile([P, 3, P], U32, name="c_rest", tag="z_bf2", align_bytes=64)
+            score(0, a, b, bank, c_first[:])
+        c_rest = sb("c_rest", [P, TILES - 1, P], U32, tag="z_bf2")
         nc.vector.tensor_copy(
-            c_rest[:].rearrange("p t (c i) -> p c t i", i=4), c_words.rearrange("p (c i t) -> p c t i", t=4, i=4)[:, :, 1:, :]
+            c_rest[:].rearrange("p t (c i) -> p c t i", i=4),
+            c_words.rearrange("p (c i t) -> p c t i", t=TILES, i=4)[:, :, 1:, :],
         )
-        for t in range(1, 4):
-            score(t, 0, S, f"bank{t}", c_rest[:, t - 1, :])
+        for t in range(1, TILES):
+            score(t, 0, S, t, c_rest[:, t - 1, :])
 
-        out_rows = out_0.rearrange("(p t) j -> p t j", t=4)
+        out_rows = out_0.rearrange("(p t) j -> p t j", t=TILES)
         out_words = out_1[0].rearrange("p n t -> p (n t)").bitcast(I32)
-        o_bf = [sb(f"o_bf{i}", [P, b - a, 4], BF16) for i, (a, b) in enumerate(PIECES)]
+        o_bf = [sb(f"o_bf{i}", [P, b - a, TILES], BF16) for i, (a, b) in enumerate(PIECES)]
         o_words = sb("o_words", [P, S], U32)
         o_scales = sb("o_scales", [P, S], U8)
-        g3 = sb("g3", [P, 4, S], F32)
-        g4 = sb("g4", [P, 4, S], F32)
-        res = sb("res", [P, 4, S], F32)
+        by_n3 = sb("by_n3", [P, TILES, S], F32)
+        by_n4 = sb("by_n4", [P, TILES, S], F32)
+        res = sb("res", [P, TILES, S], F32)
+        st_win = steps
+        m_plain, gain_over_m, m_turned = hi, lo, term_a
 
-        def fetch3(t):
-            nc.vector.tensor_copy(g3[:, t, :], win[t][:].indirect(n3_t[:]))
+        def fetch_s(t):
+            nc.vector.tensor_copy(by_n3[:, t, :], win[t][:].indirect(n3_t[:]))
 
-        def larger(t):
-            nc.vector.tensor_tensor(uv[t][:, :S], win[t][:, :S], g3[:, t, :], ALU.min if t < 2 else ALU.max)
+        def make_st(t):
+            nc.vector.tensor_tensor(st_win[t][:, :S], win[t][:, :S], by_n3[:, t, :], ALU.min if t < 2 else ALU.max)
 
-        def fetch4(t, a, b):
-            nc.vector.tensor_copy(g4[:, t, a:b], uv[t][:].indirect(n4_t[:, a // 16 : b // 16]))
+        def fetch_st(t, a, b):
+            nc.vector.tensor_copy(by_n4[:, t, a:b], st_win[t][:].indirect(n4_t[:, a // 16 : b // 16]))
 
-        def smaller(t, a, b):
-            nc.vector.tensor_tensor(res[:, t, a:b], uv[t][:, a:b], g4[:, t, a:b], ALU.min)
+        def make_out(t, a, b):
+            nc.vector.tensor_tensor(res[:, t, a:b], st_win[t][:, a:b], by_n4[:, t, a:b], ALU.min)
 
         def interleave(copy, i):
             a, b = PIECES[i]
             copy(o_bf[i][:].rearrange("p (c i) t -> p c t i", i=4), res[:, :, a:b].rearrange("p t (c i) -> p c t i", i=4))
 
-        def smaller_by_sums(t):
-            nc.vector.tensor_tensor(g4[:, t, :], uv[t][:].indirect(n4_t[:]), hi[t][:], ALU.subtract)
-            nc.scalar.activation(lo[t][:], g4[:, t, :], RELU)
-            sums = psum.tile([P, 4, P], F32, name=f"out_sum{t}", tag=f"bank{4 + 2 * t}")
-            back = psum.tile([P, 4, P], F32, name=f"out_back{t}", tag=f"bank{5 + 2 * t}")
-            for c in range(4):
-                for n, term in enumerate((hi[t], lo[t])):
-                    nc.tensor.matmul(
-                        sums[:, c, :], term[:, c * P : (c + 1) * P], identity[:], start=n == 0, stop=n == 1, is_transpose=True
-                    )
-            return sums, back
-
-        def turn_out(t, sums, back):
-            nc.scalar.copy(spread[t][:], sums[:].rearrange("j c p -> j (c p)"))
-            for c in range(4):
-                nc.tensor.transpose(back[:, c, :], spread[t][:, c * P : (c + 1) * P], identity[:])
-
-        def store_turned(t, back):
-            nc.scalar.activation(res[:, t, :], back[:].rearrange("p c j -> p (c j)"), COPY, scale=-1.0)
-            nc.sync.dma_start(out_rows[:, t, :], res[:, t, :])
-
-        def hand_on(i):
+        def quantise_out(i):
             a, b = PIECES[i]
             nc.vector.quantize_mx(
                 out=o_words[:, a:b].bitcast(FP8X4), scales=o_scales[:, a:b], in_=o_bf[i][:].rearrange("p j t -> p (j t)")
             )
 
-        fetch3(0)
-        fetch3(1)
+        fetch_s(0)
+        fetch_s(1)
         for t in range(2):
-            larger(t)
-            nc.scalar.copy(hi[t][:], uv[t][:, :S])
-        fetch3(2)
-        banks = [smaller_by_sums(t) for t in range(2)]
+            make_st(t)
+            nc.scalar.copy(m_plain[t][:], st_win[t][:, :S])
+        fetch_s(2)
+        out_sum, out_back = [], []
         for t in range(2):
-            turn_out(t, *banks[t])
+            nc.vector.tensor_tensor(by_n4[:, t, :], st_win[t][:].indirect(n4_t[:]), m_plain[t][:], ALU.subtract)
+            nc.scalar.activation(gain_over_m[t][:], by_n4[:, t, :], RELU)
+            out_sum.append(bank_tile(f"out_sum{t}", [P, 4, P], 4 + 2 * t))
+            out_back.append(bank_tile(f"out_back{t}", [P, 4, P], 5 + 2 * t))
+            for c in range(4):
+                add_turned(out_sum[t][:, c, :], (m_plain[t], gain_over_m[t]), c)
         for t in range(2):
-            store_turned(t, banks[t][1])
-        larger(2)
-        fetch3(3)
-        fetch4(2, 0, HALF)
-        larger(3)
-        for i, (a, b) in enumerate(((0, HALF), (HALF, S))):
-            if i == 1:
-                fetch4(2, a, b)
-            else:
-                smaller(2, a, b)
-            fetch4(3, a, b)
-            if i == 1:
-                smaller(2, a, b)
-            smaller(3, a, b)
-            interleave(nc.scalar.copy, i)
-            nc.sync.dma_start(out_rows[:, 2:4, a:b], res[:, 2:4, a:b])
-        hand_on(0)
+            nc.scalar.copy(m_turned[t][:], out_sum[t][:].rearrange("j c p -> j (c p)"))
+            for c in range(4):
+                nc.tensor.transpose(out_back[t][:, c, :], m_turned[t][:, c * P : (c + 1) * P], identity[:])
+        for t in range(2):
+            nc.scalar.activation(res[:, t, :], out_back[t][:].rearrange("p c j -> p (c j)"), COPY, scale=-1.0)
+            nc.sync.dma_start(out_rows[:, t, :], res[:, t, :])
+
+        make_st(2)
+        fetch_s(3)
+        fetch_st(2, 0, HALF)
+        make_st(3)
+        make_out(2, 0, HALF)
+        fetch_st(3, 0, HALF)
+        make_out(3, 0, HALF)
+        interleave(nc.scalar.copy, 0)
+        nc.sync.dma_start(out_rows[:, 2:, :HALF], res[:, 2:, :HALF])
+        for t in (2, 3):
+            fetch_st(t, HALF, S)
+        for t in (2, 3):
+            make_out(t, HALF, S)
+        interleave(nc.scalar.copy, 1)
+        nc.sync.dma_start(out_rows[:, 2:, HALF:], res[:, 2:, HALF:])
+        quantise_out(0)
         nc.sync.dma_start(out_words[:, :HALF], o_words[:, :HALF].bitcast(I32))
         interleave(nc.vector.tensor_copy, 2)
-        hand_on(1)
-        hand_on(2)
+        quantise_out(1)
+        quantise_out(2)
         nc.sync.dma_start(out_words[:, HALF:], o_words[:, HALF:].bitcast(I32))
         for q in range(4):
             queue = nc.scalar if q % 2 == 0 else nc.sync

@@ -48,7 +48,7 @@ def tile_picked_hcandrangehopmn_none_po_kernel(
             return tile
 
         xs = sb("xs", [P, T], U8, tag="x_scales_then_words")
-        w1s_raw = sb("w1s_raw", [P, S], U8)
+        w1s_raw = sb("w1s_raw", [P, S], U8, tag="w1_scales_then_gains")
         q_scales = sb("q_scales", [P, S], U8)
         c_scales = sb("c_scales", [P, S], U8)
         w1w_raw = sb("w1w_raw", [P, 2 * S], U8)
@@ -62,11 +62,9 @@ def tile_picked_hcandrangehopmn_none_po_kernel(
             nc.scalar.dma_start(w1s_raw[b:P:4, :].bitcast(I32), rows.unsqueeze(1).to_broadcast([4, 8, S // 4]))
         offs_t = load_list("offs_t", offs)
         nc.sync.dma_start(xs[:].bitcast(I32), x_scales[0].bitcast(I32).unsqueeze(1).to_broadcast([16, 8, T // 4]))
-        x_rows = x_words[0].rearrange("p n t -> p (n t)").bitcast(I32)
-        nc.sync.dma_start(xw[:, : T // 2].bitcast(I32), x_rows[:, : T // 2])
         cand_t = load_list("cand_t", cand)
         n1_t = load_list("n1_t", n1)
-        nc.sync.dma_start(xw[:, T // 2 :].bitcast(I32), x_rows[:, T // 2 :])
+        nc.sync.dma_start(xw[:].bitcast(I32), x_words[0].rearrange("p n t -> p (n t)").bitcast(I32))
         n2_t = load_list("n2_t", n2)
         n3_t = load_list("n3_t", n3)
         n4_t = load_list("n4_t", n4)
@@ -86,8 +84,8 @@ def tile_picked_hcandrangehopmn_none_po_kernel(
         deal(w1w[:].bitcast(U16), w1w_raw[:].bitcast(U16))
         deal(w1s[:], w1s_raw[:])
 
-        gains = sb("gains", [P, TILES], F32)
-        nc.gpsimd.dma_start(gains[:], gs.rearrange("(p t) o -> p (t o)", t=TILES))
+        gains = sb("gains", [P, TILES], F32, tag="w1_scales_then_gains")
+        nc.sync.dma_start(gains[:], gs.rearrange("(p t) o -> p (t o)", t=TILES))
         sign = sb("sign", [P, TILES], F32)
         hi_weight = sb("hi_weight", [P, TILES], F32)
         lo_weight = sb("lo_weight", [P, TILES], F32)
@@ -166,32 +164,40 @@ def tile_picked_hcandrangehopmn_none_po_kernel(
 
         sum_bank = [bank_tile(f"sum{c}", [P, TILES, P], c) for c in range(4)]
         turned = [sb(f"turned{c}", [P, 2, 2 * P], BF16) for c in range(4)]
-        for c in (2, 3):
-            nc.vector.memset(turned[c][:, 1, :], 0.0)
         back_bank = [bank_tile(f"back{h}", [P, 2, 2, P], 4 + h) for h in range(2)]
 
-        def add_turned(acc, terms, c):
-            for n, term in enumerate(terms):
-                nc.tensor.matmul(
-                    acc, term[:, c * P : (c + 1) * P], identity[:], start=n == 0, stop=n == len(terms) - 1, is_transpose=True
-                )
+        def add_turned(acc, terms, n, c):
+            nc.tensor.matmul(
+                acc, terms[n][:, c * P : (c + 1) * P], identity[:], start=n == 0, stop=n == len(terms) - 1, is_transpose=True
+            )
 
         def sum_z(t, chunks):
             a, b = chunks[0] * P, (chunks[-1] + 1) * P
             nc.scalar.activation(term_a[t][:, a:b], hi[t][:, a:b], COPY, scale=hi_weight[:, t : t + 1])
             nc.scalar.activation(term_b[t][:, a:b], lo[t][:, a:b], COPY, scale=lo_weight[:, t : t + 1])
-            for c in chunks:
-                add_turned(sum_bank[c][:, t, :], (y_plain[t], term_a[t][:], term_b[t][:]), c)
+            for n in range(3):
+                for c in chunks:
+                    add_turned(sum_bank[c][:, t, :], (y_plain[t], term_a[t][:], term_b[t][:]), n, c)
 
-        def turn_back(u, chunks, members):
+        def turn_back(u, chunks):
             for c in chunks:
                 nc.scalar.activation(
-                    turned[c][:, u, :].rearrange("j (p e) -> j p e", e=2)[:, :, :members],
-                    sum_bank[c][:, 2 * u : 2 * u + members, :].rearrange("j e p -> j p e"),
+                    turned[c][:, u, :].rearrange("j (p e) -> j p e", e=2),
+                    sum_bank[c][:, 2 * u : 2 * u + 2, :].rearrange("j e p -> j p e"),
                     COPY,
                     scale=0.5,
                 )
                 nc.tensor.transpose(back_bank[c // 2][:, c % 2, u, :], turned[c][:, u, :].bitcast(F32), identity[:])
+
+        def weigh(t, a, b):
+            stt(term_a[t][:, a:b], lo[t][:, a:b], lo_over_hi[:, t : t + 1], hi[t][:, a:b], ALU.mult, ALU.add)
+
+        def finish(t, a, b):
+            stt(term_b[t][:, a:b], term_a[t][:, a:b], hi_weight[:, t : t + 1], y_plain[t][:, a:b], ALU.mult, ALU.add)
+
+        def round_z(t, i):
+            a, b = PIECES[i]
+            nc.scalar.activation(z_bf[i][:, :, t], term_b[t][:, a:b], COPY, scale=0.5)
 
         def z_pairs(i):
             return z_bf[i][:].rearrange("p j t -> p (j t)").bitcast(F32).rearrange("p (j u) -> p j u", u=2)
@@ -219,29 +225,31 @@ def tile_picked_hcandrangehopmn_none_po_kernel(
         step(2, 0, 0, S)
         extremes(1, 0, S)
         sum_z(1, range(4))
-        turn_back(0, range(4), 2)
+        turn_back(0, range(4))
+        for i in (1, 2):
+            nc.scalar.copy(z_pairs(i)[:, :, 0], back_bank[1][:, i - 1, 0, :])
         step(2, 1, 0, S)
         step(3, 0, 0, HALF)
         extremes(2, 0, S)
-        sum_z(2, range(4))
+        sum_z(2, range(2))
         step(3, 1, 0, HALF)
-        step(3, 0, HALF, S)
+        weigh(2, HALF, S)
         extremes(3, 0, HALF)
-        turn_back(1, (2, 3), 1)
         sum_z(3, range(2))
-        for i in (1, 2):
-            nc.scalar.copy(z_pairs(i), back_bank[1][:, i - 1, :, :].rearrange("p u j -> p j u"))
+        step(3, 0, HALF, S)
+        finish(2, HALF, S)
         step(3, 1, HALF, S)
-        turn_back(1, range(2), 2)
+        turn_back(1, range(2))
+        round_z(2, 1)
         nc.scalar.copy(z_pairs(0).rearrange("p (c j) u -> p c j u", c=2), back_bank[0][:].rearrange("p c u j -> p c j u"))
+        round_z(2, 2)
         for a, b in PIECES[1:]:
             extremes(3, a, b)
         for a, b in PIECES[1:]:
-            stt(term_a[3][:, a:b], lo[3][:, a:b], lo_over_hi[:, 3:4], hi[3][:, a:b], ALU.mult, ALU.add)
+            weigh(3, a, b)
         for i in (1, 2):
-            a, b = PIECES[i]
-            stt(term_b[3][:, a:b], term_a[3][:, a:b], hi_weight[:, 3:4], y_plain[3][:, a:b], ALU.mult, ALU.add)
-            nc.scalar.activation(z_bf[i][:, :, 3], term_b[3][:, a:b], COPY, scale=0.5)
+            finish(3, *PIECES[i])
+            round_z(3, i)
         for i, bank in enumerate((6, 7, 0)):
             a, b = PIECES[i]
             nc.vector.quantize_mx(
@@ -302,7 +310,8 @@ def tile_picked_hcandrangehopmn_none_po_kernel(
             out_sum.append(bank_tile(f"out_sum{t}", [P, 4, P], 4 + 2 * t))
             out_back.append(bank_tile(f"out_back{t}", [P, 4, P], 5 + 2 * t))
             for c in range(4):
-                add_turned(out_sum[t][:, c, :], (m_plain[t], gain_over_m[t]), c)
+                for n in range(2):
+                    add_turned(out_sum[t][:, c, :], (m_plain[t], gain_over_m[t]), n, c)
         for t in range(2):
             nc.scalar.copy(m_turned[t][:], out_sum[t][:].rearrange("j c p -> j (c p)"))
             for c in range(4):

@@ -175,9 +175,12 @@ def tile_picked_hcandrangehopmn_none_po_kernel(
             a, b = chunks[0] * P, (chunks[-1] + 1) * P
             nc.scalar.activation(term_a[t][:, a:b], hi[t][:, a:b], COPY, scale=hi_weight[:, t : t + 1])
             nc.scalar.activation(term_b[t][:, a:b], lo[t][:, a:b], COPY, scale=lo_weight[:, t : t + 1])
-            for n in range(3):
-                for c in chunks:
-                    add_turned(sum_bank[c][:, t, :], (y_plain[t], term_a[t][:], term_b[t][:]), n, c)
+            terms = (y_plain[t], term_a[t][:], term_b[t][:])
+            for c in chunks:
+                add_turned(sum_bank[c][:, t, :], terms, 0, c)
+            for c in chunks:
+                for n in (1, 2):
+                    add_turned(sum_bank[c][:, t, :], terms, n, c)
 
         def turn_back(u, chunks):
             for c in chunks:
@@ -213,7 +216,7 @@ def tile_picked_hcandrangehopmn_none_po_kernel(
                 start=True,
                 stop=True,
             )
-            nc.scalar.activation(win[t][:, a:b], acc[:], COPY, scale=-SCORE_SCALE if t < 2 else SCORE_SCALE)
+            nc.scalar.activation(win[t][:, a:b], acc[:], COPY, scale=-SCORE_SCALE if t == 0 else SCORE_SCALE)
 
         step(0, 0, 0, HALF)
         step(0, 0, HALF, S)
@@ -273,13 +276,13 @@ def tile_picked_hcandrangehopmn_none_po_kernel(
         by_n4 = sb("by_n4", [P, TILES, S], F32)
         res = sb("res", [P, TILES, S], F32)
         st_win = steps
-        m_plain, gain_over_m, m_turned = hi, lo, term_a
+        m_plain, excess, m_turned = hi[0], lo[0], term_a[0]
 
         def fetch_s(t):
             nc.vector.tensor_copy(by_n3[:, t, :], win[t][:].indirect(n3_t[:]))
 
         def make_st(t):
-            nc.vector.tensor_tensor(st_win[t][:, :S], win[t][:, :S], by_n3[:, t, :], ALU.min if t < 2 else ALU.max)
+            nc.vector.tensor_tensor(st_win[t][:, :S], win[t][:, :S], by_n3[:, t, :], ALU.min if t == 0 else ALU.max)
 
         def fetch_st(t, a, b):
             nc.vector.tensor_copy(by_n4[:, t, a:b], st_win[t][:].indirect(n4_t[:, a // 16 : b // 16]))
@@ -299,28 +302,27 @@ def tile_picked_hcandrangehopmn_none_po_kernel(
 
         fetch_s(0)
         fetch_s(1)
-        for t in range(2):
-            make_st(t)
-            nc.scalar.copy(m_plain[t][:], st_win[t][:, :S])
+        make_st(0)
+        nc.scalar.copy(m_plain[:], st_win[0][:, :S])
+        make_st(1)
         fetch_s(2)
-        out_sum, out_back = [], []
-        for t in range(2):
-            nc.vector.tensor_tensor(by_n4[:, t, :], st_win[t][:].indirect(n4_t[:]), m_plain[t][:], ALU.subtract)
-            nc.scalar.activation(gain_over_m[t][:], by_n4[:, t, :], RELU)
-            out_sum.append(bank_tile(f"out_sum{t}", [P, 4, P], 4 + 2 * t))
-            out_back.append(bank_tile(f"out_back{t}", [P, 4, P], 5 + 2 * t))
-            for c in range(4):
-                for n in range(2):
-                    add_turned(out_sum[t][:, c, :], (m_plain[t], gain_over_m[t]), n, c)
-        for t in range(2):
-            nc.scalar.copy(m_turned[t][:], out_sum[t][:].rearrange("j c p -> j (c p)"))
-            for c in range(4):
-                nc.tensor.transpose(out_back[t][:, c, :], m_turned[t][:, c * P : (c + 1) * P], identity[:])
-        for t in range(2):
-            nc.scalar.activation(res[:, t, :], out_back[t][:].rearrange("p c j -> p (c j)"), COPY, scale=-1.0)
-            nc.sync.dma_start(out_rows[:, t, :], res[:, t, :])
-
+        nc.vector.tensor_tensor(by_n4[:, 0, :], st_win[0][:].indirect(n4_t[:]), m_plain[:], ALU.subtract)
+        nc.scalar.activation(excess[:], by_n4[:, 0, :], RELU)
+        out_sum = bank_tile("out_sum", [P, 4, P], 4)
+        out_back = bank_tile("out_back", [P, 4, P], 5)
+        for c in range(4):
+            for n in range(2):
+                add_turned(out_sum[:, c, :], (m_plain, excess), n, c)
+        nc.scalar.copy(m_turned[:], out_sum[:].rearrange("j c p -> j (c p)"))
+        for c in range(4):
+            nc.tensor.transpose(out_back[:, c, :], m_turned[:, c * P : (c + 1) * P], identity[:])
+        nc.scalar.activation(res[:, 0, :], out_back[:].rearrange("p c j -> p (c j)"), COPY, scale=-1.0)
+        nc.sync.dma_start(out_rows[:, 0, :], res[:, 0, :])
+        fetch_st(1, 0, S)
         make_st(2)
+        make_out(1, 0, S)
+        nc.sync.dma_start(out_rows[:, 1, :], res[:, 1, :])
+
         fetch_s(3)
         fetch_st(2, 0, HALF)
         make_st(3)

from contextlib import ExitStack

import concourse.mybir as mybir
from concourse.masks import make_identity

F32 = mybir.dt.float32
BF16 = mybir.dt.bfloat16
I32 = mybir.dt.int32
U32 = mybir.dt.uint32
U16 = mybir.dt.uint16
U8 = mybir.dt.uint8
FP8X4 = mybir.dt.float8_e4m3fn_x4
FP4X4 = mybir.dt.float4_e2m1fn_x4
ALU = mybir.AluOpType
COPY = mybir.ActivationFunctionType.Copy
RELU = mybir.ActivationFunctionType.Relu
SIGN = mybir.ActivationFunctionType.Sign

P = 128
T = 2048
S = 512
HALF = S // 2
TILES = 4
SCORE_SCALE = 0.0625
PIECES = ((0, HALF), (HALF, HALF + P), (HALF + P, S))
HALVES = ((0, HALF), (HALF, S))
FLOPS = 2 * 2 * 512 * 512 * 512


def tile_picked_hcandrangehopmn_none_po_kernel(
    tc, x_words, x_scales, w1_words, w1_scales, gs, offs, n1, n2, cand, n3, n4, out_0, out_1, out_2
):
    nc = tc.nc
    with ExitStack() as ctx:
        lists = ctx.enter_context(tc.tile_pool(name="lists", bufs=1))
        keep = ctx.enter_context(tc.tile_pool(name="keep", bufs=1))
        psum = ctx.enter_context(tc.psum_pool(name="psum", bufs=1))

        def sb(name, shape, dtype, tag=None):
            return keep.tile(shape, dtype, name=name, tag=tag or name, align_bytes=64)

        def bank_tile(name, shape, bank):
            return psum.tile(shape, F32, name=name, tag=f"bank{bank}")

        def load_list(name, src):
            tile = lists.tile([P, S // 16], U16, name=name)
            nc.sync.dma_start(tile[:], src)
            return tile

        xs = sb("xs", [P, T], U8, tag="x_scales_then_words")
        w1s_raw = sb("w1s_raw", [P, S], U8, tag="w1_scales_then_gains")
        q_scales = sb("q_scales", [P, S], U8)
        c_scales = sb("c_scales", [P, S], U8)
        w1w_raw = sb("w1w_raw", [P, 2 * S], U8)
        xw = sb("xw", [P, T], U32)
        win = [sb(f"win{t}", [P, 2 * S], F32) for t in range(TILES)]
        last_plain = sb("last_plain", [P, S], F32)

        nc.sync.dma_start(w1w_raw[:].bitcast(I32), w1_words[0].bitcast(I32))
        for b in range(4):
            rows = w1_scales[0, b:16:4, :].bitcast(I32)
            nc.scalar.dma_start(w1s_raw[b:P:4, :].bitcast(I32), rows.unsqueeze(1).to_broadcast([4, 8, S // 4]))
        offs_t = load_list("offs_t", offs)
        nc.sync.dma_start(xs[:].bitcast(I32), x_scales[0].bitcast(I32).unsqueeze(1).to_broadcast([16, 8, T // 4]))
        cand_t = load_list("cand_t", cand)
        n1_t = load_list("n1_t", n1)
        nc.sync.dma_start(xw[:].bitcast(I32), x_words[0].rearrange("p n t -> p (n t)").bitcast(I32))
        n2_t = load_list("n2_t", n2)
        n3_t = load_list("n3_t", n3)
        n4_t = load_list("n4_t", n4)
        nc.vector.memset(q_scales[:].bitcast(I32), 0)
        nc.vector.memset(c_scales[:].bitcast(I32), 0)
        nc.vector.memset(win[0][:, S:], 0.0)

        def move_rows(queue, dst, src):
            for q in range(4):
                queue.dma_start(dst[32 * q : 32 * q + 4, :].bitcast(I32), src[32 * q : 32 * q + 32 : 8, :].bitcast(I32))

        def deal(dst, src):
            nc.vector.tensor_copy(dst.rearrange("p (t m) -> p t m", t=TILES), src.rearrange("p (m t) -> p t m", t=TILES))

        w1w = sb("w1w", [P, 2 * S], U8)
        w1s = sb("w1s", [P, S], U8)
        deal(w1w[:].bitcast(U16), w1w_raw[:].bitcast(U16))
        deal(w1s[:], w1s_raw[:])

        gains = sb("gains", [P, TILES], F32, tag="w1_scales_then_gains")
        nc.sync.dma_start(gains[:], gs.rearrange("(p t) o -> p (t o)", t=TILES))
        sign = sb("sign", [P, TILES], F32)
        hi_weight = sb("hi_weight", [P, TILES], F32)
        lo_weight = sb("lo_weight", [P, TILES], F32)
        lo_over_hi = sb("lo_over_hi", [P, TILES], F32)
        nc.scalar.activation(sign[:], gains[:], SIGN)
        nc.scalar.activation(hi_weight[:], sign[:], COPY, scale=1.5, bias=0.5)
        nc.scalar.activation(lo_weight[:], sign[:], COPY, scale=-1.5, bias=0.5)
        nc.scalar.activation(lo_over_hi[:], sign[:], COPY, scale=0.75, bias=-1.25)
        identity = sb("identity", [P, P], F32)
        make_identity(nc, identity[:])

        q_bytes = sb("q_bytes", [P, S], U8)
        c_bytes = sb("c_bytes", [P, S], U8)
        nc.vector.tensor_copy(q_bytes[:], xs[:].indirect(offs_t[:]))
        move_rows(nc.scalar, q_scales, q_bytes)
        nc.vector.tensor_copy(c_bytes[:], xs[:].indirect(cand_t[:]))

        c_bytes_dealt = sb("c_bytes_dealt", [P, S], U8)
        c_first = sb("c_first", [P, P], U32)
        words = sb("words", [P, 2 * S], U32, tag="x_scales_then_words")
        q_words = words[:, :S]
        c_words = words[:, S:]
        deal(c_bytes_dealt[:], c_bytes[:])
        nc.vector.tensor_copy(q_words, xw[:].indirect(offs_t[:]))

        y_plain = [win[1][:, S:], win[2][:, S:], win[3][:, S:], last_plain[:]]

        def project(t, a, b, bank):
            acc = bank_tile(f"y{t}_{a}", [P, b - a], bank)
            nc.tensor.matmul_mx(
                out=acc[:],
                lhsT=w1w[:, 2 * P * t : 2 * P * (t + 1)].bitcast(FP4X4),
                lhsT_scale=w1s[:, P * t : P * (t + 1)],
                rhs=q_words[:, a:b].bitcast(FP8X4),
                rhs_scale=q_scales[:, a:b],
                start=True,
                stop=True,
            )
            return acc

        def leave(dst, acc, t):
            nc.scalar.activation(dst, acc[:], COPY, scale=gains[:, t : t + 1])

        first = [project(0, 0, HALF, 0), project(0, HALF, S, 4)]
        for dst in (win[0], y_plain[0]):
            for (a, b), acc in zip(HALVES, first):
                leave(dst[:, a:b], acc, 0)
        for t in range(1, TILES):
            acc = project(t, 0, S, t)
            leave(win[t][:, :S], acc, t)
            leave(y_plain[t], acc, t)

        nc.vector.tensor_copy(c_words, xw[:].indirect(cand_t[:]))
        nc.vector.tensor_copy(c_first[:], c_words.rearrange("p (m t) -> p m t", t=TILES)[:, :, 0])
        move_rows(nc.sync, c_scales, c_bytes_dealt)

        z_bf = [sb(f"z_bf{i}", [P, b - a, TILES], BF16) for i, (a, b) in enumerate(PIECES)]
        z_words = sb("z_words", [P, S], U32)
        z_scales = sb("z_scales", [P, S], U8)
        steps = [sb(f"steps{t}", [P, 2 * S], F32) for t in range(TILES)]
        hi = [sb(f"hi{t}", [P, S], F32) for t in range(TILES)]
        lo = [sb(f"lo{t}", [P, S], F32) for t in range(TILES)]
        term_a = [sb(f"term_a{t}", [P, S], F32) for t in range(TILES)]
        term_b = [sb(f"term_b{t}", [P, S], F32) for t in range(TILES)]
        stt = nc.vector.scalar_tensor_tensor

        def step(t, side, a, b):
            entries = (n1_t, n2_t)[side][:, a // 16 : b // 16]
            nc.vector.tensor_tensor(
                steps[t][:, side * S + a : side * S + b], win[t][:].indirect(entries), y_plain[t][:, a:b], ALU.subtract
            )

        def extremes(t, a, b):
            stt(hi[t][:, a:b], steps[t][:, a:b], 0.0, steps[t][:, S + a : S + b], ALU.max, ALU.max)
            stt(lo[t][:, a:b], steps[t][:, a:b], 0.0, steps[t][:, S + a : S + b], ALU.min, ALU.min)

        sum_bank = [bank_tile(f"sum{c}", [P, TILES, P], c) for c in range(4)]
        turned = [sb(f"turned{c}", [P, 2, 2 * P], BF16) for c in range(4)]
        back_bank = [bank_tile(f"back{h}", [P, 2, 2, P], 4 + h) for h in range(2)]

        def add_turned(acc, terms, n, c):
            nc.tensor.matmul(
                acc, terms[n][:, c * P : (c + 1) * P], identity[:], start=n == 0, stop=n == len(terms) - 1, is_transpose=True
            )

        def sum_z(t, chunks):
            a, b = chunks[0] * P, (chunks[-1] + 1) * P
            nc.scalar.activation(term_a[t][:, a:b], hi[t][:, a:b], COPY, scale=hi_weight[:, t : t + 1])
            nc.scalar.activation(term_b[t][:, a:b], lo[t][:, a:b], COPY, scale=lo_weight[:, t : t + 1])
            terms = (y_plain[t], term_a[t][:], term_b[t][:])
            for c in chunks:
                add_turned(sum_bank[c][:, t, :], terms, 0, c)
            for c in chunks:
                for n in (1, 2):
                    add_turned(sum_bank[c][:, t, :], terms, n, c)

        def turn_back(u, chunks):
            for c in chunks:
                nc.scalar.activation(
                    turned[c][:, u, :].rearrange("j (p e) -> j p e", e=2),
                    sum_bank[c][:, 2 * u : 2 * u + 2, :].rearrange("j e p -> j p e"),
                    COPY,
                    scale=0.5,
                )
                nc.tensor.transpose(back_bank[c // 2][:, c % 2, u, :], turned[c][:, u, :].bitcast(F32), identity[:])

        def weigh(t, a, b):
            stt(term_a[t][:, a:b], lo[t][:, a:b], lo_over_hi[:, t : t + 1], hi[t][:, a:b], ALU.mult, ALU.add)

        def finish(t, a, b):
            stt(term_b[t][:, a:b], term_a[t][:, a:b], hi_weight[:, t : t + 1], y_plain[t][:, a:b], ALU.mult, ALU.add)

        def round_z(t, i):
            a, b = PIECES[i]
            nc.scalar.activation(z_bf[i][:, :, t], term_b[t][:, a:b], COPY, scale=0.5)

        def z_pairs(i):
            return z_bf[i][:].rearrange("p j t -> p (j t)").bitcast(F32).rearrange("p (j u) -> p j u", u=2)

        def score(t, a, b, bank, candidates):
            acc = bank_tile(f"s{t}_{a}", [P, b - a], bank)
            nc.tensor.matmul_mx(
                out=acc[:],
                lhsT=candidates.bitcast(FP8X4),
                lhsT_scale=c_scales[:, P * t : P * (t + 1)],
                rhs=z_words[:, a:b].bitcast(FP8X4),
                rhs_scale=z_scales[:, a:b],
                start=True,
                stop=True,
            )
            nc.scalar.activation(win[t][:, a:b], acc[:], COPY, scale=-SCORE_SCALE if t == 0 else SCORE_SCALE)

        step(0, 0, 0, HALF)
        step(0, 0, HALF, S)
        step(0, 1, 0, S)
        step(1, 0, 0, S)
        extremes(0, 0, S)
        sum_z(0, range(4))
        step(1, 1, 0, S)
        step(2, 0, 0, S)
        extremes(1, 0, S)
        sum_z(1, range(4))
        turn_back(0, range(4))
        for i in (1, 2):
            nc.scalar.copy(z_pairs(i)[:, :, 0], back_bank[1][:, i - 1, 0, :])
        step(2, 1, 0, S)
        step(3, 0, 0, HALF)
        extremes(2, 0, S)
        sum_z(2, range(2))
        step(3, 1, 0, HALF)
        weigh(2, HALF, S)
        extremes(3, 0, HALF)
        sum_z(3, range(2))
        step(3, 0, HALF, S)
        finish(2, HALF, S)
        step(3, 1, HALF, S)
        turn_back(1, range(2))
        round_z(2, 1)
        nc.scalar.copy(z_pairs(0).rearrange("p (c j) u -> p c j u", c=2), back_bank[0][:].rearrange("p c u j -> p c j u"))
        round_z(2, 2)
        for a, b in PIECES[1:]:
            extremes(3, a, b)
        for a, b in PIECES[1:]:
            weigh(3, a, b)
        for i in (1, 2):
            finish(3, *PIECES[i])
            round_z(3, i)
        for i, bank in enumerate((6, 7, 0)):
            a, b = PIECES[i]
            nc.vector.quantize_mx(
                out=z_words[:, a:b].bitcast(FP8X4), scales=z_scales[:, a:b], in_=z_bf[i][:].rearrange("p j t -> p (j t)")
            )
            score(0, a, b, bank, c_first[:])
        c_rest = sb("c_rest", [P, TILES - 1, P], U32, tag="z_bf2")
        nc.vector.tensor_copy(
            c_rest[:].rearrange("p t (c i) -> p c t i", i=4),
            c_words.rearrange("p (c i t) -> p c t i", t=TILES, i=4)[:, :, 1:, :],
        )
        for t in range(1, TILES):
            score(t, 0, S, t, c_rest[:, t - 1, :])

        out_rows = out_0.rearrange("(p t) j -> p t j", t=TILES)
        out_words = out_1[0].rearrange("p n t -> p (n t)").bitcast(I32)
        o_bf = [sb(f"o_bf{i}", [P, b - a, TILES], BF16) for i, (a, b) in enumerate(PIECES)]
        o_words = sb("o_words", [P, S], U32)
        o_scales = sb("o_scales", [P, S], U8)
        by_n3 = sb("by_n3", [P, TILES, S], F32)
        by_n4 = sb("by_n4", [P, TILES, S], F32)
        res = sb("res", [P, TILES, S], F32)
        st_win = steps
        m_plain, excess, m_turned = hi[0], lo[0], term_a[0]

        def fetch_s(t):
            nc.vector.tensor_copy(by_n3[:, t, :], win[t][:].indirect(n3_t[:]))

        def make_st(t):
            nc.vector.tensor_tensor(st_win[t][:, :S], win[t][:, :S], by_n3[:, t, :], ALU.min if t == 0 else ALU.max)

        def fetch_st(t, a, b):
            nc.vector.tensor_copy(by_n4[:, t, a:b], st_win[t][:].indirect(n4_t[:, a // 16 : b // 16]))

        def make_out(t, a, b):
            nc.vector.tensor_tensor(res[:, t, a:b], st_win[t][:, a:b], by_n4[:, t, a:b], ALU.min)

        def interleave(copy, i):
            a, b = PIECES[i]
            copy(o_bf[i][:].rearrange("p (c i) t -> p c t i", i=4), res[:, :, a:b].rearrange("p t (c i) -> p c t i", i=4))

        def quantise_out(i):
            a, b = PIECES[i]
            nc.vector.quantize_mx(
                out=o_words[:, a:b].bitcast(FP8X4), scales=o_scales[:, a:b], in_=o_bf[i][:].rearrange("p j t -> p (j t)")
            )

        fetch_s(0)
        fetch_s(1)
        make_st(0)
        nc.scalar.copy(m_plain[:], st_win[0][:, :S])
        make_st(1)
        fetch_s(2)
        nc.vector.tensor_tensor(by_n4[:, 0, :], st_win[0][:].indirect(n4_t[:]), m_plain[:], ALU.subtract)
        nc.scalar.activation(excess[:], by_n4[:, 0, :], RELU)
        out_sum = bank_tile("out_sum", [P, 4, P], 4)
        out_back = bank_tile("out_back", [P, 4, P], 5)
        for c in range(4):
            for n in range(2):
                add_turned(out_sum[:, c, :], (m_plain, excess), n, c)
        nc.scalar.copy(m_turned[:], out_sum[:].rearrange("j c p -> j (c p)"))
        for c in range(4):
            nc.tensor.transpose(out_back[:, c, :], m_turned[:, c * P : (c + 1) * P], identity[:])
        nc.scalar.activation(res[:, 0, :], out_back[:].rearrange("p c j -> p (c j)"), COPY, scale=-1.0)
        nc.sync.dma_start(out_rows[:, 0, :], res[:, 0, :])
        fetch_st(1, 0, S)
        make_st(2)
        make_out(1, 0, S)
        nc.sync.dma_start(out_rows[:, 1, :], res[:, 1, :])

        fetch_s(3)
        fetch_st(2, 0, HALF)
        make_st(3)
        make_out(2, 0, HALF)
        fetch_st(3, 0, HALF)
        make_out(3, 0, HALF)
        interleave(nc.scalar.copy, 0)
        nc.sync.dma_start(out_rows[:, 2:, :HALF], res[:, 2:, :HALF])
        for t in (2, 3):
            fetch_st(t, HALF, S)
        for t in (2, 3):
            make_out(t, HALF, S)
        interleave(nc.scalar.copy, 1)
        nc.sync.dma_start(out_rows[:, 2:, HALF:], res[:, 2:, HALF:])
        quantise_out(0)
        nc.sync.dma_start(out_words[:, :HALF], o_words[:, :HALF].bitcast(I32))
        interleave(nc.vector.tensor_copy, 2)
        quantise_out(1)
        quantise_out(2)
        nc.sync.dma_start(out_words[:, HALF:], o_words[:, HALF:].bitcast(I32))
        for q in range(4):
            queue = nc.scalar if q % 2 == 0 else nc.sync
            queue.dma_start(out_2[0, 4 * q : 4 * q + 4, :].bitcast(I32), o_scales[32 * q : 32 * q + 4, :].bitcast(I32))
